import numpy as np, ml_dtypes
CORES = [2,6,10,14,18,22,26,30]
N = 8
BF = ml_dtypes.bfloat16
W, E, B, C, RO, NC = 2048, 1024, 128, 10, 3, 32
def group(rng, noise, good, mode, proto):
    n = W // NC; mem = rng.permutation(W).reshape(NC, n); cl = np.zeros(W, np.int64); cl[mem] = np.arange(NC)[:, None]
    x = np.minimum(np.maximum(proto[:, cl] + rng.integers(-noise, noise + 1, (16, W)), 0), 63)
    nx = rng.integers(0, NC, (16, NC))
    if mode == 1: nx[:] = np.arange(NC)
    if mode == 2: nx[:] = cl[0]
    if mode == 3: nx[:] = cl[W - 1]
    l = mem[nx[:, cl], rng.integers(0, n, (16, W))]
    if mode == 1: l[:] = np.arange(W)
    if mode == 2: l[:] = 0
    if mode == 3: l[:] = W - 1
    i = np.zeros((16, E), np.int64); q = rng.integers(0, NC, E)
    for k in range(16):
        i[k] = mem[q, rng.integers(0, n, E)]
        if k < 15:
            go = nx[k, q]; q = np.where(good[k], go, (go + rng.integers(1, NC, E)) % NC)
    return x, i, l
def parts(rng, style):
    x = np.zeros((N, 8, 16, W), np.int64); i = np.zeros((N, 8, 16, E), np.int64); l = np.zeros((N, 8, 16, W), np.int64)
    for a in range(N):
        for g in range(8):
            noise = int(rng.integers(1, 4)); mode = 0; proto = rng.integers(0, 64, (16, NC))
            good = rng.random((15, E)) < rng.choice(np.array([0.2, 0.6, 0.8, 0.95, 1.0]), E)
            if style == "ties": noise = 0; proto = 16 + 8 * rng.integers(0, 2, (16, NC))
            if style == "corners":
                noise = 0; mode = (a + g) % 4; n = rng.choice(np.array([0, 1, C - 1, C, C + 1, 15]), E)
                good = np.argsort(np.argsort(rng.random((15, E)), axis=0), axis=0) < n
            x[a, g], i[a, g], l[a, g] = group(rng, noise, good, mode, proto)
    t = np.stack([rng.integers(20, 70, (N, 8, 16)), rng.integers(200, 420, (N, 8, 16))], axis=-1)
    return x, rng.integers(0, 64, (N, 8, 16, E)), i, l, rng.integers(0, 64, (N, 8, 16, B)), rng.integers(0, 256, (N, 8, 16, 1)), rng.integers(0, 2048, (N, 8, 16, 2)), t
def pack(x, gs, i, l, z, w, h, t):
    def bf(v): return np.ascontiguousarray(v.reshape(N, 128, -1)).astype(np.float32).astype(BF)
    def whole(v): return np.ascontiguousarray(v.reshape(N, 128, -1)).astype(np.int32)
    return {"xc": bf(x), "gi": bf(gs), "ix": whole(i), "lk": whole(l), "zc": bf(z), "wt": whole(w), "hk": whole(h), "th": whole(t)}
def ends(rng, lo, hi, shape, share):
    v = np.where(rng.random(shape) < 0.5, lo, hi)
    return np.where(rng.random(shape) < share, v, rng.integers(lo, hi + 1, shape))
def records(rng, n):
    k = rng.integers(0, 3, (N, 8, 1, n))
    return np.where(k == 0, 0, np.where(k == 1, 63, ends(rng, 0, 63, (N, 8, 16, n), 1.0)))
def full(rng, p):
    u = rng.permutation(4096); f, k = np.unique(((u * u >> 5) + p * u) & (E - 1), return_index=True)
    return u[rng.permutation(k)[:B]]
def setup_inputs(rng):
    return pack(*parts(rng, "plain"))
def setup_inputs_ties(rng):
    x, gs, i, l, z, w, h, t = parts(rng, "ties")
    gs = 16 + 8 * rng.integers(0, 2, gs.shape); z = 16 + 8 * rng.integers(0, 2, z.shape)
    t = rng.choice(np.array([56, 63, 64, 65, 72]), t.shape)
    for a in range(N):
        for g in (6, 7):
            v = (256, 257, 259, 513, 515, 767, 1005, 1007)[(a + g) & 7]; base = int(rng.integers(0, 1008 - v))
            m = rng.permutation(W); low = np.flatnonzero(m < W // 2); high = np.flatnonzero(m >= W // 2)
            size = base + np.where(m < W // 2, 0, v + (rng.random(W) < 0.3).astype(np.int64))
            x[a, g] = (size >> 4) + (np.arange(16)[:, None] < (size & 15)).astype(np.int64)
            i[a, g] = low[rng.integers(0, W // 2, (16, E))]; l[a, g] = high[rng.integers(0, W // 2, (16, W))]
            t[a, g, :, 0] = v; t[a, g, :, 1] = 1008
    return pack(x, gs, i, l, z, w, h, t)
def setup_inputs_corners(rng):
    x, gs, i, l, z, w, h, t = parts(rng, "corners")
    for a in range(N):
        for g in range(8):
            kind = (3 * a + g) % 4
            if kind == 0: w[a, g] = 255
            if kind == 1: w[a, g] = 255 * rng.integers(0, 2, (16, 1))
            if kind == 2: w[a, g] = 0; w[a, g, 15] = 1
            t[a, g, :, 0] = (0, 1, 40, 0, 0, 1008, 40, 1)[(a + g) % 8]
            t[a, g, :, 1] = rng.choice(np.array([0, 340, 1008]), 16)
            h[a, g] = np.where(rng.random((16, 2)) < 0.4, 2047 * rng.integers(0, 2, (16, 2)), h[a, g])
    k = rng.integers(0, 4, (N, 8, 1, B)); z = np.where(k == 0, 0, np.where(k == 1, 63, z))
    k = rng.integers(0, 4, (N, 8, 1, E)); gs = np.where(k == 0, 0, np.where(k == 1, 63, gs))
    i = np.where(rng.random((N, 8, 1, E)) < 0.1, (W - 1) * rng.integers(0, 2, (N, 8, 1, E)), i)
    return pack(x, gs, i, l, z, w, h, t)
def setup_inputs_crowd(rng):
    x, gs, i, l, z, w, h, t = parts(rng, "plain")
    w[:, 0::4] = 0; w[:, 0::4, 5] = 1; z[:, 0::4, 5] = rng.integers(0, 6, (N, 2, B)); h[:, 0::4, :, 0] = 0
    i[:, 1] = rng.choice(np.array([0, 1, W // 2, W - 2, W - 1]), (N, 16, E)); gs[:, 1] = 30
    w[:, 2] = 0
    z[:, 3] = z[:, 3][..., rng.integers(0, 3, B)]
    for a in range(N):
        for g in (5, 6, 7):
            w[a, g] = 0; w[a, g, 0] = 1; w[a, g, 1] = 64; gs[a, g] = 0
            p = int(h[a, g, 0, 0]); u = full(rng, p)
            if g == 5: u[B // 2:] = u[:B // 2]
            z[a, g, 0] = u & 63; z[a, g, 1] = u >> 6
            e = ((u * u >> 5) + p * u) & (E - 1)
            if g == 5:
                side = rng.random(B // 2) < 0.5; side[0] = True; side[1] = False; near = np.concatenate([side, ~side])
                x[a, g] = rng.integers(16, 25, (16, W)); i[a, g] = rng.integers(0, W, (16, E))
                z[a, g, 2:] = np.where(near, rng.integers(16, 25, (14, B)), rng.integers(56, 64, (14, B)))
                t[a, g, :, 0] = 0; t[a, g, :, 1] = rng.integers(206, 448, 16)
            if g == 6:
                o = rng.permutation(W); i[a, g][:, e] = o[(np.arange(16)[:, None] % (W // B)) * B + np.arange(B)]
                t[a, g, :, 0] = 0
            if g == 7: t[a, g, :, 0] = 1008
    t[2, :, :, 0] = 0
    gs[2, 3] = 30; c = int(rng.integers(0, W)); u = np.add.reduce(w[2, 3] * z[2, 3], axis=0) & 4095
    e = ((u * u >> 5) + h[2, 3, 0, 0] * u) & (E - 1)
    i[2, 3][:, e] = c; l[2, 3][:, c] = c
    return pack(x, gs, i, l, z, w, h, t)
def setup_inputs_spread(rng):
    x, gs, i, l, z, w, h, t = parts(rng, "plain")
    x = x >> rng.integers(0, 7, (N, 8, 1, W)); gs = gs >> rng.integers(0, 7, (N, 8, 1, E)); z = z >> rng.integers(0, 7, (N, 8, 1, B))
    i[:, ::2] = (W * rng.random((N, 4, 16, E)) ** 3).astype(np.int64); l[:, ::4] = (W * rng.random((N, 2, 16, W)) ** 3).astype(np.int64)
    w = np.exp2(8 * rng.random(w.shape)).astype(np.int64); h = np.exp2(11 * rng.random(h.shape)).astype(np.int64)
    t = np.minimum(np.exp2(10.2 * rng.random(t.shape)).astype(np.int64), 1008)
    return pack(x, gs, i, l, z, np.minimum(w, 255), np.minimum(h, 2047), t)
def setup_inputs_ends(rng):
    x = records(rng, W); gs = records(rng, E); z = records(rng, B)
    x[:, 0::2, :, 0] = 63; x[:, 0::2, :, W - 1] = 0; x[:, 1::2, :, 0] = 0; x[:, 1::2, :, W - 1] = 63
    i = ends(rng, 0, W - 1, (N, 8, 16, E), 0.75); l = ends(rng, 0, W - 1, (N, 8, 16, W), 0.75)
    w = ends(rng, 0, 255, (N, 8, 16, 1), 0.75); w[:, 7] = 255
    h = ends(rng, 0, 2047, (N, 8, 16, 2), 0.8); t = ends(rng, 0, 1008, (N, 8, 16, 2), 1.0)
    t[0, :, :, 0] = 1008; a = N - 1; t[a, 7, :, 0] = 0
    i[0, 5] = W - 1; l[0, 5, :, W - 1] = 0
    t[1, :, :, 0] = 1008; t[1, 6, :, 0] = 0
    w[1, 6] = 0; w[1, 6, 15] = 255; z[1, 6, 15] = 0; z[1, 6, 15, B - 1] = 63; h[1, 6, :, 0] = 2047 * rng.integers(0, 2, 16)
    i[1, 6] = W - 1; i[1, 6, :, 0] = 0; l[1, 6, :, 0] = 0; l[1, 6, :, W - 1] = 0
    v = z[a, 7]; v[:, B - 1] = 63; v[:, B - 2] = 0; v[15, B - 2] = 63; v[:, B - 3] = 0; v[:4, B - 3] = 63; v[4, B - 3] = 5
    h[a, 7, 0, 0] = 2047; h[a, 7, 1, 0] = 0; h[a, 7, 15, 1] = 2047
    h[a, 7, 15, 0] = ((E - 1 - (3777 * 3777 >> 5)) * pow(3777, -1, E)) % E
    c = ((3088 * 3088 >> 5) + h[a, 7, :, 0] * 3088) & (E - 1)
    gs[a, 7][:, c] = 0; gs[a, 7, :, E - 1] = v[:, B - 2]
    i[a, 7, :, c[1]] = 0; i[a, 7, :, c[0]] = W - 1; i[a, 7, :8, E - 1] = 0; i[a, 7, 8:, E - 1] = W - 1
    l[a, 7, :, 0] = 0; l[a, 7, :, W - 1] = 0
    return pack(x, gs, i, l, z, w, h, t)
def check_inputs(d):
    bad = []
    for k, lo, hi in (("xc", 0, 63), ("gi", 0, 63), ("ix", 0, W - 1), ("lk", 0, W - 1), ("zc", 0, 63), ("wt", 0, 255), ("hk", 0, 2047), ("th", 0, 1008)):
        v = np.asarray(d[k]).astype(np.float64)
        if not np.all((v >= lo) & (v <= hi) & (v == np.floor(v))): bad.append("range of " + k)
    return bad
def reference(xc, gi, ix, lk, zc, wt, hk, th):
    def cut(v): return np.asarray(v).astype(np.float32).astype(np.int64).reshape(N, 8, 16, -1)
    X, G, I, L, Z, w, h, t = cut(xc), cut(gi), cut(ix), cut(lk), cut(zc), cut(wt), cut(hk), cut(th)
    A = np.zeros(N, np.int64); lane = np.arange(B)
    for rnd in range(RO):
        count = np.zeros(N, np.int64)
        for a in range(N):
            r = (a - rnd) % N
            for g in range(8):
                z = Z[r, g]
                u = np.add.reduce(w[a, g] * z, axis=0) & 4095
                em = ((u * u >> 5) + h[a, g, :, 0:1] * u + A[a]) & (E - 1)
                d = np.add.reduce(np.abs(G[a, g][:, em] - z[:, None, :]), axis=0)
                e = em[np.argmin(d, axis=0), lane]
                J = I[a, g][:, e]
                x = X[a, g][:, J]
                y = X[a, g][:, np.take_along_axis(L[a, g], J, 1)]
                s = np.add.reduce(np.abs(y[:, :15] - x[:, 1:]), axis=0)
                far = np.add.reduce(np.abs(x - z[:, None, :]), axis=0)
                rec = np.add.reduce((s <= t[a, g, :15, 0:1]).astype(np.int64), axis=0) >= C
                fresh = ((u * u >> 4) + h[a, g, :, 1:2] * u) & (W - 1)
                col = np.where(rec[None, :] | (far > t[a, g, :, 1:2]), fresh, J)
                ks = np.argmax(s, axis=0)
                f, first = np.unique(e, return_index=True)
                I[a, g][:, f] = col[:, first]
                if rnd < RO - 1:
                    o = first[rec[first]]; G[a, g][:, e[o]] = z[:, o]
                q = np.flatnonzero(~rec); c, one = np.unique(J[ks[q], q], return_index=True); q = q[one]
                L[a, g][ks[q], c] = J[ks[q] + 1, q]
                count[a] += np.count_nonzero(rec)
                Z[r, g] = (z + np.maximum.reduce(x, axis=1)) >> 1
        A = count
    return {"yz": Z.reshape(N, 128, B).astype(np.float32).astype(BF), "yi": I.reshape(N, 128, E).astype(np.float32), "yl": L.reshape(N, 128, W).astype(np.float32)}

@@ -1,0 +1,528 @@
+from concourse.mybir import AluOpType, ActivationFunctionType
+
+ALU = AluOpType
+ACT = ActivationFunctionType
+RO = 3
+SEG = [8 * c * (c + 1) for c in range(9)]
+PSUM = ("p0", "p1", "p2", "p3", "p4", "p5", "p6", "p7")
+SCRATCH = {b: ("psum", [128, 512], "float32") for b in PSUM}
+for _t, _names in {
+    "float32": "IX:1152 LK:2192 ONES:128 IDF:128 BOF:128 SHF:128 HALF:128 RQ:128 M16:128 RMIN:128 RMAX:128 UT:128 MKEY:128 JJ0:128 JJ1:128 ACC:1 WLF:64 SG:128 HV:128 "
+               "NT:128 REP2:128 NOH:128 JN:128 TOLD:128",
+    "bfloat16": "XC:2048 GI:1152 Z0:128 Z1:128 Z2:128 ZR:128 ZN0:128 ZN1:128 ZN2:128 ZH:128 ZS:2048 ZREP:2048 ZT0:128 ZT1:128 RM:2048 ONESB:512 IDB:128 NIDB:128 HID:128 NHID:128 IDK:128 "
+                "NID4K:128 BOB:128 SHB:128 EB:144 G8A:8 G8B:8 C8:8 C8H:8 EIGHT:8 MROW:128 M24:128 M16B:128 MNEG:128 SEL:2048 RX:2048 RD:576 R1:576 R2:576 R3:576 WB:128 "
+                "DG:2048 AG:2048 GR:1024 XG:2064 XM:2048 CMP:128 RECS:128 RBS:128 XA:576 XS:576 AF:2048 NOHB:128",
+    "float16": "PD:128 QD:128 PW:128 QW:128 VH:128 ERM:128 ERU:128 ERM2:128 ERU2:128 JH:128 LG:2048",
+    "int32": "IXI:1024 LKI:2048 WTI:1 HKI:2 THI:2 PIO:16 PR:16 CIO:8 PWI:128 QWI:128 UI:128 UU:128 S5:128 BS:128 VQ:128 EI:128 EM:128 KMIN:128 KA:8 KMX:128 KJ:24",
+    "uint16": "OFFG:8 ENDS:2 EU:128 E8U:8 JU:128 NU:128 GOFF:8 NOFF:8 LOFF:8 JX8:8",
+}.items():
+    for _n in _names.split():
+        SCRATCH[_n.split(":")[0]] = ("sbuf", [128, int(_n.split(":")[1])], _t)
+PART = {}
+_at = 0
+for _n in "RF:1 WC:1 HKF:2 ACOL:1 BCOL:1 THF:2 JJC:1 NM15:1 M95:1 ENDF:4 MK:16 NC8:8 DUMPI:8 DUMPL:8".split():
+    PART[_n.split(":")[0]] = _at
+    _at += int(_n.split(":")[1])
+SCRATCH["CF"] = ("sbuf", [128, _at], "float32")
+SEMAPHORES = ["sv", "ss", "sp", "sg", "ls", "za1", "za2", "zr"] + ["d%d" % i for i in range(14)]
+TWO = ("bfloat16", "float16", "uint16")
+COST = dict(cy=1.0, pe=0.5, ga=1.5, sc=3.0, wake=60.0, same=40.0, dma=2000.0, rem=2500.0)
+TRIALS = 250
+ORDER = {}
+
+
+def R(buf, c0, c1, step=1, p0=0, p1=128):
+    if buf in PART:
+        return ("CF", PART[buf] + c0, PART[buf] + c1, step, p0, p1)
+    return (buf, c0, c1, step, p0, p1)
+
+
+def ind(win, off): return ("ind", win, off)
+def wid(r): return 16 * (r[2][2] - r[2][1]) if len(r) == 3 else (r[2] - r[1] + r[3] - 1) // r[3]
+def kind(r): return SCRATCH[(r[1] if len(r) == 3 else r)[0]][2]
+
+
+def schedule(ops, seed):
+    n = len(ops)
+    rnd = [seed * 7919 + 12345]
+
+    def rand():
+        rnd[0] = (rnd[0] * 1103515245 + 12345) & 0x7fffffff
+        return rnd[0] / 0x7fffffff
+
+    succ = [[] for _ in range(n)]
+    left = [0] * n
+    for i, o in enumerate(ops):
+        for j, w in o["pre"].items():
+            succ[j].append((i, w))
+            left[i] += 1
+    pri = [0.0] * n
+    for i in range(n - 1, -1, -1):
+        o = ops[i]
+        for k, w in succ[i]:
+            d = o["cost"] + (o["lat"] + COST["wake" if ops[k]["q"] != o["q"] else "same"] if w else 0)
+            if d + pri[k] > pri[i]: pri[i] = d + pri[k]
+        if not succ[i]: pri[i] = o["cost"] + o["lat"]
+    amp = 0.0 if seed == 0 else 1500.0 * rand()
+    key = [p + amp * (rand() - 0.5) for p in pri]
+    look = 0.0 if seed == 0 else 300.0 * rand()
+    ready = {}
+    rt = [0.0] * n
+    free = {}
+    for i in range(n):
+        if not left[i]: ready.setdefault(ops[i]["q"], []).append(i)
+    order = []
+    end = 0.0
+    while len(order) < n:
+        bq, bt = None, 1e18
+        for q, L in ready.items():
+            if L:
+                t = max(free.get(q, 0.0), min(rt[i] for i in L))
+                if t < bt: bq, bt = q, t
+        L = ready[bq]
+        best = max((i for i in L if rt[i] <= bt + look), key=lambda i: key[i])
+        L.remove(best)
+        o = ops[best]
+        s = max(bt, rt[best])
+        e = s + o["cost"]
+        free[bq] = e
+        order.append(best)
+        end = max(end, e + o["lat"])
+        for k, w in succ[best]:
+            a = e + o["lat"] + COST["wake" if ops[k]["q"] != bq else "same"] if w else s
+            if a > rt[k]: rt[k] = a
+            left[k] -= 1
+            if not left[k]: ready.setdefault(ops[k]["q"], []).append(k)
+    return end, order
+
+
+def make(g, T):
+    eng = {"V": g.vector, "S": g.scalar, "P": g.tensor, "G": g, "Y": g.sync}
+    own = {"V": "sv", "S": "ss", "P": "sp", "G": "sg"}
+    ops, hist = [], {}
+
+    def ap(r):
+        if len(r) == 3:
+            return ap(r[1]).indirect(ap(r[2]))
+        b, c0, c1, s, p0, p1 = r
+        return T[b][p0:p1, c0:c1] if s == 1 else T[b][p0:p1, c0:c1:s]
+
+    def add(q, outs, ins, call, cost, lat=0.0, sem=None, inc=1, extra=()):
+        i = len(ops)
+        acc = []
+        for r in ins:
+            if isinstance(r, tuple):
+                acc += [(r[1], False), (r[2], False)] if len(r) == 3 else [(r, False)]
+        for r in outs:
+            acc += [(r[1], True), (r[2], False)] if len(r) == 3 else [(r, True)]
+        pre = {j: True for j in extra}
+        for r, w in acc:
+            ps = r[0] in PSUM
+            h = hist.setdefault(r[0], [])
+            for (j, r2, w2) in h:
+                if j == i: continue
+                q2 = ops[j]["q"]
+                if ps:
+                    if q == q2 == "P": wait = False
+                    elif q == q2 and not (w or w2): continue
+                    else: wait = not (q == q2 and not w2)
+                else:
+                    if not (w or w2) or r[1] >= r2[2] or r2[1] >= r[2] or r[4] >= r2[5] or r2[4] >= r[5]: continue
+                    if r[3] == r2[3] and r[3] > 1 and (r[1] - r2[1]) % r[3]: continue
+                    wait = not (q == q2 and not w2)
+                pre[j] = pre.get(j, False) or wait
+            if ps and q == "P": h[:] = []
+            elif w and not ps and r[3] == 1:
+                h[:] = [a for a in h if a[0] == i or not (a[1][1] >= r[1] and a[1][2] <= r[2] and a[1][4] >= r[4] and a[1][5] <= r[5])]
+            h.append((i, r, w))
+        ops.append(dict(q=q, call=call, cost=float(cost), lat=float(lat), pre=pre, sem=sem or own.get(q), inc=inc))
+        return i
+
+    def sc(x): return ap(x) if isinstance(x, tuple) else x
+
+    def vcost(out, in_, f):
+        n = wid(out)
+        if len(out) == 3: return 50 + n * COST["sc"] * COST["cy"]
+        if len(in_) == 3: return 50 + n * COST["ga"] * COST["cy"]
+        return max(64, n * f) * COST["cy"]
+
+    def half(*rs): return 0.5 if all(kind(r) in TWO for r in rs) else 1.0
+
+    def cp(out, in_): add("V", [out], [in_], lambda n: n.tensor_copy(ap(out), ap(in_)), vcost(out, in_, half(out, in_)))
+
+    def tt(out, a, b, o):
+        add("V", [out], [a, b], lambda n: n.tensor_tensor(ap(out), ap(a), ap(b), o), vcost(out, a, 1.0 if a[0] in PSUM or b[0] in PSUM else 2.0))
+
+    def ts(out, a, s1, o1, s2=None, o2=None):
+        c = vcost(out, a, half(out, a))
+        if o2 is None: add("V", [out], [a, s1], lambda n: n.tensor_scalar(ap(out), ap(a), sc(s1), None, o1), c)
+        else: add("V", [out], [a, s1, s2], lambda n: n.tensor_scalar(ap(out), ap(a), sc(s1), sc(s2), o1, o2), c)
+
+    def scan(out, a, b, o1, o2):
+        add("V", [out], [a, b], lambda n: n.tensor_tensor_scan(ap(out), ap(a), ap(b), 0.0, o1, o2), vcost(out, a, half(out, a, b)))
+
+    def fill(out, v): add("V", [out], [], lambda n: n.memset(ap(out), v), vcost(out, out, half(out)))
+
+    def act(out, in_, f, bias=0.0, scale=1.0, acc=None):
+        c = 65 + wid(out) * COST["ga"] * COST["cy"] if len(in_) == 3 else max(64, wid(out)) * COST["cy"]
+        if acc is None: add("S", [out], [in_, bias, scale], lambda n: n.activation(ap(out), ap(in_), f, bias=sc(bias), scale=sc(scale)), c)
+        else: add("S", [out, acc], [in_, bias, scale], lambda n: n.activation(ap(out), ap(in_), f, bias=sc(bias), scale=sc(scale), accum_out=ap(acc)), c + 20)
+
+    def mm(*group):
+        def call(n):
+            for (o, l, r, a, b) in group:
+                x = n.matmul(ap(o), ap(l), ap(r), a, b)
+            return x
+        c = sum(max(min(64, wid(l)), wid(r)) * (4 if kind(l) == "float32" else 1) for (o, l, r, a, b) in group) * COST["pe"]
+        add("P", [x[0] for x in group], [x[1] for x in group] + [x[2] for x in group], call, c)
+
+    def iota(out, pat, base, cm): add("G", [out], [], lambda n: n.iota(ap(out), pat, base, cm, allow_small_or_imprecise_dtypes=True), 130 + 2 * wid(out))
+    def asel(out, in_, pat, o, fillv, base, cm): add("G", [out], [in_], lambda n: n.affine_select(ap(out), ap(in_), pat, o, fillv, base, cm), 170 + 2 * wid(out))
+
+    nd = [0]
+
+    def dma(q, out, in_):
+        sem = "d%d" % nd[0]
+        nd[0] += 1
+        o = T[out][:] if isinstance(out, str) else ap(out)
+        i = T[in_][:] if isinstance(in_, str) else ap(in_)
+        s = in_ if isinstance(out, str) else out
+        by = wid(s) * 128 * (2 if kind(s) in TWO else 4)
+        add(q, [] if isinstance(out, str) else [out], [] if isinstance(in_, str) else [in_], lambda n: n.dma_start(o, i), 60, COST["dma"] + by / 200.0, sem, 16)
+
+    def send(out, in_, rsem, dst, src, topo):
+        rid, pid, _ = topo.addr(dst)
+        en = topo.engines(src, dst)[:8]
+        i = add("G", [], [in_], lambda n: n.remote_dma(ap(out), ap(in_), T.sem[rsem], T.sem["ls"], pid, rid, sum(1 << x for x in en)), 1000, COST["rem"], "ls", len(en))
+        add("net", [out], [], None, 0, 0, rsem, len(en), (i,))
+
+    def run():
+        if not ORDER:
+            best = min((schedule(ops, s) for s in range(TRIALS)), key=lambda x: x[0])
+            ORDER["best"] = best
+        cnt, known, tok = {}, {q: {} for q in eng}, {}
+        for i in ORDER["best"][1]:
+            o = ops[i]
+            q = o["q"]
+            cnt[o["sem"]] = cnt.get(o["sem"], 0) + o["inc"]
+            if q == "net":
+                tok[i] = (o["sem"], cnt[o["sem"]], {})
+                continue
+            k = known[q]
+            waits = sorted((tok[j] for j, w in o["pre"].items() if w), key=lambda t: (t[0], -t[1]))
+            waits.sort(key=lambda t: t[0] == o["sem"])
+            for (s, v, snap) in waits:
+                if k.get(s, 0) < v:
+                    eng[q].wait_ge(T.sem[s], v)
+                    k[s] = v
+                    for a, b in snap.items():
+                        if k.get(a, 0) < b: k[a] = b
+            c = o["call"](eng[q])
+            if o["sem"] != "ls": c.then_inc(T.sem[o["sem"]], o["inc"])
+            tok[i] = (o["sem"], cnt[o["sem"]], dict(k))
+        for s in sorted(cnt):
+            if known["G"].get(s, 0) < cnt[s]: g.wait_ge(T.sem[s], cnt[s])
+
+    return dict(cp=cp, tt=tt, ts=ts, scan=scan, fill=fill, act=act, mm=mm, iota=iota, asel=asel, dma=dma, send=send, run=run)
+
+
+def rank_program(g, core, T, topo):
+    rank = T.rank_of(core)
+    if rank is None:
+        return
+    n = len(T.cores)
+    m = make(g, T)
+    cp, tt, ts, scan, fill, act, mm, iota, asel, dma = (m[k] for k in ("cp", "tt", "ts", "scan", "fill", "act", "mm", "iota", "asel", "dma"))
+    F = lambda b: R(b, 0, SCRATCH[b][1][1])
+    C = lambda b, i=0: R(b, i, i + 1)
+    S8 = lambda i: R("WLF", 8 * i, 8 * i + 8)
+    K8 = lambda i: R("KJ", 8 * i, 8 * i + 8)
+    D8 = lambda b: R(b, 0, 8)
+    PU, PP, PQ, PZ = R("p0", 0, 128), R("p0", 128, 256), R("p0", 256, 384), R("p0", 384, 512)
+    KEY, E8, REC8, AA = R("p1", 0, 128), R("p1", 128, 136), R("p1", 136, 144), R("p1", 144, 145)
+    CNT, CNB, JJB = R("p3", 128, 256), R("p3", 256, 384), R("p3", 384, 512)
+    ST, FT = R("p4", 128, 256), R("p4", 256, 384)
+    J8, CN8 = R("p7", 96, 104), R("p7", 104, 112)
+    HP, DP, JNP = R("p7", 128, 256), R("p7", 256, 384), R("p7", 384, 512)
+    WI, WL, WX, WG = F("IX"), F("LK"), F("XC"), F("GI")
+
+    dma("Y", F("Z0"), "zc"); dma("Y", F("WTI"), "wt"); dma("Y", F("HKI"), "hk")
+    dma("S", R("GI", 0, 1024), "gi"); dma("Y", F("IXI"), "ix"); dma("Y", F("LKI"), "lk"); dma("S", F("XC"), "xc"); dma("Y", F("THI"), "th")
+
+    fill(F("ONES"), 1.0)
+    iota(F("PIO"), [[0, 16]], 0, 1)
+    asel(F("IDF"), F("ONES"), [[-1, 128]], ALU.is_equal, 0.0, 0, 1)
+    asel(F("BOF"), F("ONES"), [[-16, 8], [0, 16]], ALU.is_ge, 0.0, 0, 1)
+    asel(F("BOF"), F("BOF"), [[16, 8], [0, 16]], ALU.is_ge, 0.0, 15, -1)
+    iota(F("RQ"), [[0, 8], [1, 16]], 0, 0)
+    iota(F("CIO"), [[1, 8]], 0, 0)
+    asel(F("SHF"), F("ONES"), [[-1, 128]], ALU.is_equal, 0.0, -1, 1)
+    asel(F("UT"), F("BOF"), [[1, 128]], ALU.is_ge, 0.0, 0, -1)
+    fill(F("ZS"), 0.0)
+    for h in (0, 1):
+        fill(R("RX", 1024 * h, 1024 * h + 1024), 1.0)
+    fill(R("RX", 0, 2048, 16), 0.0)
+    fill(F("ONESB"), 1.0)
+    fill(F("EB"), 0.0)
+    for q in (0, 3, 1, 2):
+        asel(R("RM", 512 * q, 512 * q + 512), F("ONESB"), [[-1, 32], [0, 16]], ALU.is_equal, 0.0, -32 * q, 1)
+    for c in range(8):
+        asel(R("R1", SEG[c], SEG[c + 1]), R("ONESB", 0, 16 * c + 16), [[-1, 16 * c + 16]], ALU.is_equal, 0.0, 0, 1)
+    ts(F("PR"), F("PIO"), 15, ALU.bitwise_and)
+    act(F("BOB"), F("BOF"), ACT.Copy)
+    cp(C("RF"), C("PR"))
+    act(F("IDB"), F("IDF"), ACT.Copy)
+    act(F("NIDB"), F("IDF"), ACT.Copy, scale=-1.0)
+    cp(C("WC"), C("WTI"))
+    ts(F("WB"), F("BOF"), C("WC"), ALU.mult)
+    cp(R("HKF", 0, 2), F("HKI"))
+    ts(F("PD"), F("IDF"), C("HKF", 0), ALU.mult)
+    ts(F("QD"), F("IDF"), C("HKF", 1), ALU.mult)
+    PA, PB = R("p1", 128, 256), R("p1", 256, 384)
+    mm((PA, F("BOB"), F("PD"), True, True), (PB, F("BOB"), F("QD"), True, True))
+    ts(F("PWI"), PA, C("WC"), ALU.mult)
+    ts(F("QWI"), PB, C("WC"), ALU.mult)
+    ts(F("PWI"), F("PWI"), 1023, ALU.bitwise_and)
+    ts(F("QWI"), F("QWI"), 2047, ALU.bitwise_and)
+    cp(F("PW"), F("PWI"))
+    cp(F("QW"), F("QWI"))
+    ts(R("MK", 0, 16), R("RQ", 0, 16), C("RF"), ALU.is_equal)
+    ts(F("M16"), F("RQ"), C("RF"), ALU.is_equal)
+    ts(F("RMIN"), F("RQ"), 0.0, ALU.is_equal, 3.0e7, ALU.mult)
+    ts(F("RMAX"), F("RMIN"), -2.0, ALU.mult, 3.0e7, ALU.add)
+    act(F("G8A"), R("BOF", 0, 128, 16), ACT.Copy, scale=16384.0)
+    act(F("G8B"), R("BOF", 0, 128, 16), ACT.Copy, scale=32768.0)
+    act(F("C8"), R("BOF", 0, 128, 16), ACT.Copy)
+    act(F("C8H"), R("BOF", 0, 128, 16), ACT.Copy, scale=-0.5)
+    cp(F("OFFG"), F("CIO"))
+    act(F("MROW"), F("RQ"), ACT.Copy, scale=1024.0)
+    ts(C("JJC"), C("RF"), -2048.0, ALU.mult, 30720.0, ALU.add)
+    fill(R("IX", 1024, 1152), 0.0)
+    fill(R("LK", 2048, 2192), 0.0)
+    fill(R("GI", 1024, 1152), 0.0)
+    fill(R("XG", 2048, 2064), 0.0)
+    act(F("M16B"), F("M16"), ACT.Copy)
+    for k in range(16):
+        act(R("SEL", 128 * k, 128 * k + 128), F("IDF"), ACT.Copy, scale=C("MK", k))
+    act(R("EB", 15, 143, 16), R("BOF", 0, 128, 16), ACT.Copy)
+    ts(D8("NC8"), R("BOF", 0, 128, 16), -1.0, ALU.mult)
+    for c in range(8):
+        act(R("R2", SEG[c], SEG[c + 1]), R("ONESB", 0, 16 * c + 16), ACT.Copy, scale=C("NC8", c))
+    fill(F("R3"), 0.0)
+    for c in range(8):
+        act(R("R3", SEG[c + 1] - 16, SEG[c + 1]), R("UT", 16 * c, 16 * c + 16), ACT.Copy, scale=4096.0)
+    fill(F("RD"), 0.0)
+    for c in range(8):
+        fill(C("RD", SEG[c]), 1.0e6)
+    ts(C("ENDF", 0), C("RF"), 7.0, ALU.min)
+    ts(C("ENDF", 1), C("ENDF", 0), 8.0, ALU.mult, 24.0, ALU.add)
+    tt(C("ENDF", 2), C("ENDF", 0), C("ENDF", 1), ALU.mult)
+    ts(C("ENDS"), C("ENDF", 2), 15.0, ALU.add)
+    ts(D8("DUMPI"), F("CIO"), 16.0, ALU.mult, C("RF"), ALU.add)
+    ts(D8("DUMPL"), D8("DUMPI"), 2049.0, ALU.add)
+    ts(D8("DUMPI"), D8("DUMPI"), 1024.0, ALU.add)
+    ts(F("MNEG"), F("M16"), 128.0, ALU.mult, -128.0, ALU.add)
+    cp(R("THF", 0, 2), F("THI"))
+    ts(C("NM15"), C("RF"), 15.0, ALU.is_equal, 2000.0, ALU.mult)
+    tt(C("ACOL"), C("THF", 0), C("NM15"), ALU.subtract)
+    ts(C("BCOL"), C("THF", 1), -1.0, ALU.mult, 1023.5, ALU.add)
+    act(F("HID"), F("IDF"), ACT.Copy, scale=0.5)
+    act(F("NHID"), F("IDF"), ACT.Copy, scale=-0.5)
+    act(F("IDK"), F("IDF"), ACT.Copy, scale=512.0)
+    act(F("NID4K"), F("IDF"), ACT.Copy, scale=-4096.0)
+    act(F("SHB"), F("SHF"), ACT.Copy)
+    fill(F("EIGHT"), -7.0)
+    fill(F("M24"), -16777216.0)
+    fill(F("HALF"), 0.5)
+    fill(C("M95"), -9.5)
+    cp(R("IX", 0, 1024), F("IXI"))
+
+    def ustage(t):
+        z = F("Z%d" % t)
+        mm((PU, F("WB"), z, True, True), (PP, F("PW"), z, True, True), (PQ, F("QW"), z, True, True))
+        cp(F("UI"), PU)
+        ts(F("UI"), F("UI"), 4095, ALU.bitwise_and)
+        tt(F("UU"), F("UI"), F("UI"), ALU.mult)
+        ts(F("S5"), F("UU"), 5, ALU.arith_shift_right, 1023, ALU.bitwise_and)
+        tt(F("BS"), PP, F("S5"), ALU.add)
+        ts(F("VQ"), F("UU"), 4, ALU.arith_shift_right, 2047, ALU.bitwise_and)
+        tt(F("VQ"), PQ, F("VQ"), ALU.add)
+        ts(F("VQ"), F("VQ"), 2047, ALU.bitwise_and)
+        cp(F("VH"), F("VQ"))
+        cp(R("ZS", 0, 2048, 16), z)
+        scan(R("ZREP", 512, 1536), R("RX", 512, 1536), R("ZS", 512, 1536), ALU.mult, ALU.add)
+        mm((R("p0", 384, 512), z, F("NIDB"), True, True))
+        act(F("ZT%d" % (t & 1)), R("p0", 384, 512), ACT.Copy)
+
+    def estage(t):
+        b = F("BS")
+        if t:
+            ts(F("EI"), b, AA, ALU.add, 8192.0, ALU.add)
+            b = F("EI")
+        ts(F("EM"), b, 1023, ALU.bitwise_and)
+        cp(F("EU"), F("EM"))
+        cp(F("MKEY"), F("EM"))
+        mm((KEY, F("MKEY"), F("IDF"), True, False))
+
+    def zsub(p, t, a, b): return (p, F("ZT%d" % (t & 1)), R("RM", a, b), True, False)
+
+    def dist(win, off, sub, sh, who, t=None):
+        bank = ["p2", "p5"]
+        for q in range(4):
+            a, b = 512 * q, 512 * q + 512
+            if who[q] == "S":
+                p = bank.pop(0)
+                x = 512 * (p == "p5")
+                act(R("GR", x, x + 512), ind(win, R(off, 32 * q, 32 * q + 32)), ACT.Copy)
+                P = R(p, 0, 512)
+                if sub == "ZREP": mm(zsub(P, t, a, b))
+                else: mm((P, F("NIDB"), R(sub, a + sh, b + sh), True, False))
+                mm((P, F("IDB"), R("GR", x, x + 512), False, True))
+                act(R("AG", a, b), R(p, 0, 512), ACT.Abs)
+            else:
+                tt(R("DG", a, b), ind(win, R(off, 32 * q, 32 * q + 32)), R(sub, a + sh, b + sh), ALU.subtract)
+                act(R("AG", a, b), R("DG", a, b), ACT.Abs)
+
+    def gstage(t):
+        dist(WG, "EU", "ZREP", 0, "SVVS", t)
+        for q in (0, 1, 2, 3):
+            mm(*[(R("p1", k, 128, 16, 32 * q, 32 * q + 32), R("AG", 512 * q + k, 512 * q + 512, 16), F("G8A"), False, False) for k in range(16)])
+        mm((KEY, F("IDB"), F("MROW"), False, True))
+
+    def argstage(t):
+        scan(F("KMIN"), F("RMIN"), KEY, ALU.max, ALU.min)
+        ts(F("KA"), R("KMIN", 15, 128, 16), 1023, ALU.bitwise_and)
+        tt(F("ERM"), ind(F("KA"), F("OFFG")), F("M16"), ALU.mult)
+        mm((E8, F("ERM"), F("C8"), True, True))
+        cp(F("E8U"), E8)
+        cp(F("JU"), ind(WI, F("E8U")))
+        act(F("JJ%d" % (t & 1)), ind(WI, F("E8U")), ACT.Identity, bias=C("JJC"))
+        cp(F("JH"), F("JU"))
+
+    def lkx(t):
+        lk = F("LKI") if t == 0 else WL
+        for h in (0, 1):
+            L = 1024 * h
+            cp(R("LG", L, L + 1024), ind(lk, R("JU", 64 * h, 64 * h + 64)))
+            p = R(("p3", "p4")[h], 0, 64)
+            mm(*[(p, R("SEL", 128 * k, 128 * k + 128), R("LG", L + k, L + 1024, 16), k == 0, k == 15) for k in range(16)])
+            cp(R("NU", 64 * h, 64 * h + 64), p)
+        for q in range(4):
+            act(R("XG", 512 * q, 512 * q + 512), ind(WX, R("JU", 32 * q, 32 * q + 32)), ACT.Copy)
+
+    def pairs(masked, plain):
+        for (a, b, P) in ((0, 512, R("p6", 0, 512)), (512, 576, R("p7", 0, 64))):
+            mm((P, F("M16B"), R("R3", a, b), True, False), (P, F(plain), R("R1", a, b), False, False), (P, F(masked), R("R2", a, b), False, True))
+            act(R("XA", a, b), P, ACT.Abs)
+
+    def lost(out16):
+        scan(F("XS"), F("RD"), F("XA"), ALU.max, ALU.min)
+        ts(out16, ind(F("XS"), C("ENDS")), 0.0, ALU.is_le)
+
+    def idx(t):
+        cp(F("ERU"), ind(F("KA"), F("OFFG")))
+        pairs("ERM", "ERU")
+        lost(R("WLF", 16, 32))
+        tt(S8(0), S8(2), D8("DUMPI"), ALU.mult)
+        tt(S8(0), E8, S8(0), ALU.max)
+        cp(F("NOFF"), S8(0))
+
+    def znext(t):
+        for h in (0, 1024):
+            scan(R("XM", h, h + 1024), R("RX", h, h + 1024), R("XG", h, h + 1024), ALU.mult, ALU.max)
+        mm((PZ, F("IDB"), F("Z%d" % t), True, False), (PZ, F("IDB"), R("XM", 15, 2048, 16), False, True))
+        act(F("ZH"), PZ, ACT.Copy, bias=129.75, scale=0.5)
+        act(F("ZN%d" % t), F("ZH"), ACT.Copy, bias=-130.0)
+        if t < RO - 1:
+            m["send"](F("Z%d" % (t + 1)), F("ZN%d" % t), "za%d" % (t + 1), T.cores[(rank + 1) % n], core, topo)
+        else:
+            m["send"](F("ZR"), F("ZN%d" % t), "zr", T.cores[(rank - t) % n], core, topo)
+
+    def far(t):
+        P = R("p5", 0, 512)
+        for q in range(4):
+            a, b = 512 * q, 512 * q + 512
+            mm(zsub(P, t, a, b), (P, F("IDB"), R("XG", a, b), False, True))
+            act(R("AF", a, b), P, ACT.Abs)
+
+    def ystage(t):
+        dist(WX, "NU", "XG", 1, "VSVV")
+        for h in (0, 1):
+            mm(*[(R("p4", 128 + 64 * h, 192 + 64 * h), R("EB", 15 - k, 143 - k), R("AG", 1024 * h + k, 1024 * h + 1024, 16), k == 0, k == 14) for k in range(15)])
+
+    def rec(t):
+        ts(F("CMP"), ST, C("ACOL"), ALU.is_le)
+        if t < RO - 1:
+            mm((CNT, F("IDB"), F("MNEG"), True, False), (CNT, F("CMP"), F("BOB"), False, True))
+            act(F("RECS"), CNT, ACT.Sign, bias=C("M95"), acc=F("ACC"))
+            mm((REC8, F("IDB"), F("EIGHT"), True, False), (REC8, F("RECS"), F("C8H"), False, True), (AA, F("HALF"), F("ACC"), True, True))
+        mm((CN8, F("CMP"), F("C8"), True, True))
+        mm((CNB, F("BOB"), F("CMP"), True, True))
+
+    def gists(t):
+        tt(S8(4), REC8, D8("DUMPI"), ALU.mult)
+        tt(F("GOFF"), S8(4), S8(0), ALU.max)
+        cp(ind(WG, F("GOFF")), F("Z%d" % t))
+
+    def names(t):
+        mm((HP, F("HID"), F("VH"), True, False), (HP, F("HID"), F("JH"), False, True), (DP, F("HID"), F("VH"), True, False), (DP, F("NHID"), F("JH"), False, True))
+        act(F("HV"), HP, ACT.Copy)
+        act(F("RBS"), CNB, ACT.Sign, bias=C("M95"))
+        mm((FT, F("IDK"), F("RBS"), True, False))
+        for h in (0, 1):
+            mm(*[(R("p4", 256 + 64 * h, 320 + 64 * h), R("EB", 15 - k, 143 - k), R("AF", 1024 * h + k, 1024 * h + 1024, 16), False, False) for k in range(16)])
+        mm((FT, F("IDK"), F("RBS"), False, True))
+        act(F("SG"), FT, ACT.Sign, bias=C("BCOL"))
+        tt(F("NT"), DP, F("SG"), ALU.mult)
+        tt(ind(WI, F("NOFF")), F("HV"), F("NT"), ALU.add)
+
+    def links(t):
+        JJ = F("JJ%d" % (t & 1))
+        mm((PZ, F("IDB"), F("M24"), True, False),
+           *([(R("p0", 384 + k, 512, 16), R("AG", k, 2048, 16), F("G8B"), False, False) for k in range(15)] + [(PZ, JJ, F("IDF"), False, True)]))
+        scan(F("KMX"), F("RMAX"), PZ, ALU.min, ALU.max)
+        ts(K8(0), R("KMX", 15, 128, 16), 32767, ALU.bitwise_and)
+        ts(K8(1), R("KMX", 15, 128, 16), 2047, ALU.bitwise_and)
+        ts(S8(5), CN8, 10.0, ALU.is_ge, 2048.0, ALU.mult)
+        tt(K8(2), K8(1), S8(5), ALU.max)
+        cp(F("REP2"), ind(K8(0), F("OFFG")))
+        mm((JJB, F("REP2"), F("IDF"), True, True))
+        tt(F("ERM2"), ind(K8(2), F("OFFG")), F("M16"), ALU.mult)
+        mm((J8, F("ERM2"), F("C8"), True, True))
+        cp(F("ERU2"), ind(K8(2), F("OFFG")))
+        pairs("ERM2", "ERU2")
+        tt(F("NOH"), JJB, JJ, ALU.not_equal)
+        act(F("NOHB"), F("NOH"), ACT.Copy)
+        mm((JNP, F("SHB"), F("JH"), True, False), (JNP, F("NID4K"), F("NOHB"), False, True))
+        act(F("JN"), JNP, ACT.Copy)
+        cp(F("JX8"), J8)
+        tt(F("TOLD"), ind(WL, F("JX8")), F("NOH"), ALU.mult)
+        lost(R("WLF", 16, 32))
+        tt(S8(6), S8(2), D8("DUMPL"), ALU.mult)
+        tt(F("LOFF"), J8, S8(6), ALU.max)
+        tt(ind(WL, F("LOFF")), F("TOLD"), F("JN"), ALU.max)
+
+    ustage(0)
+    estage(0)
+    for t in range(RO):
+        gstage(t)
+        argstage(t)
+        lkx(t)
+        if t == 0:
+            for h in (0, 1024):
+                cp(R("LK", h, h + 1024), R("LKI", h, h + 1024))
+        idx(t)
+        znext(t)
+        ystage(t)
+        rec(t)
+        if t < RO - 1: gists(t)
+        far(t)
+        names(t)
+        links(t)
+        if t < RO - 1:
+            ustage(t + 1)
+            estage(t + 1)
+    dma("S", "yi", R("IX", 0, 1024))
+    dma("Y", "yl", R("LK", 0, 2048))
+    dma("Y", "yz", F("ZR"))
+    m["run"]()

@@ -10,8 +10,8 @@ for _t, _names in {
     "float32": "IX:1152 LK:2192 ONES:128 IDF:128 BOF:128 SHF:128 HALF:128 RQ:128 M16:128 RMIN:128 RMAX:128 UT:128 MKEY:128 JJ0:128 JJ1:128 ACC:1 WLF:64 SG:128 HV:128 "
                "NT:128 REP2:128 NOH:128 JN:128 TOLD:128",
     "bfloat16": "XC:2048 GI:1152 Z0:128 Z1:128 Z2:128 ZR:128 ZN0:128 ZN1:128 ZN2:128 ZH:128 ZS:2048 ZREP:2048 ZT0:128 ZT1:128 RM:2048 ONESB:512 IDB:128 NIDB:128 HID:128 NHID:128 IDK:128 "
-                "NID4K:128 BOB:128 SHB:128 EB:144 G8A:8 G8B:8 C8:8 C8H:8 EIGHT:8 MROW:128 M24:128 M16B:128 MNEG:128 SEL:2048 RX:2048 RD:576 R1:576 R2:576 R3:576 WB:128 "
-                "DG:2048 AG:2048 GR:1024 XG:2064 XM:2048 CMP:128 RECS:128 RBS:128 XA:576 XS:576 AF:2048 NOHB:128",
+                "NID4K:128 BOB:128 SHB:128 EB:432 G8:64 MROW:128 M24:128 M16B:128 MNEG:128 SEL:2048 RX:2048 RD:576 R1:576 R2:576 R3:576 WB:128 "
+                "DG:2048 AG:2048 DY:2048 AY:2048 GR:1024 XG:2064 XM:2048 CMP:128 RECS:128 RBS:128 XA:576 XS:576 AF:2048 NOHB:128",
     "float16": "PD:128 QD:128 PW:128 QW:128 VH:128 ERM:128 ERU:128 ERM2:128 ERU2:128 JH:128 LG:2048",
     "int32": "IXI:1024 LKI:2048 WTI:1 HKI:2 THI:2 PIO:16 PR:16 CIO:8 PWI:128 QWI:128 UI:128 UU:128 S5:128 BS:128 VQ:128 EI:128 EM:128 KMIN:128 KA:8 KMX:128 KJ:24",
     "uint16": "OFFG:8 ENDS:2 EU:128 E8U:8 JU:128 NU:128 GOFF:8 NOFF:8 LOFF:8 JX8:8",
@@ -26,8 +26,11 @@ for _n in "RF:1 WC:1 HKF:2 ACOL:1 BCOL:1 THF:2 JJC:1 NM15:1 M95:1 ENDF:4 MK:16 N
 SCRATCH["CF"] = ("sbuf", [128, _at], "float32")
 SEMAPHORES = ["sv", "ss", "sp", "sg", "ls", "za1", "za2", "zr"] + ["d%d" % i for i in range(14)]
 TWO = ("bfloat16", "float16", "uint16")
-COST = dict(cy=1.0, pe=0.5, ga=1.5, sc=3.0, wake=60.0, same=40.0, dma=2000.0, rem=2500.0)
-TRIALS = 250
+COSTS = [dict(cy=1.0, pe=0.5, ga=1.5, sc=3.0, wake=60.0, same=40.0, dma=2000.0, bw=200.0, rem=2500.0),
+         dict(cy=0.9, pe=0.5, ga=1.15, sc=2.0, wake=110.0, same=60.0, dma=2000.0, bw=250.0, rem=3500.0),
+         dict(cy=1.15, pe=0.6, ga=1.95, sc=5.0, wake=60.0, same=40.0, dma=2200.0, bw=150.0, rem=2000.0)]
+TRIALS = 5000
+GW, GO, YW = "SWWS", (1, 0, 2, 3), "SVVV"
 ORDER = {}
 
 
@@ -42,58 +45,91 @@ def wid(r): return 16 * (r[2][2] - r[2][1]) if len(r) == 3 else (r[2] - r[1] + r
 def kind(r): return SCRATCH[(r[1] if len(r) == 3 else r)[0]][2]
 
 
-def schedule(ops, seed):
+def schedule(ops):
     n = len(ops)
-    rnd = [seed * 7919 + 12345]
+    rnd = [12345]
 
     def rand():
         rnd[0] = (rnd[0] * 1103515245 + 12345) & 0x7fffffff
-        return rnd[0] / 0x7fffffff
+        return (rnd[0] >> 8) / 0x7fffff
 
+    que = [o["q"] for o in ops]
     succ = [[] for _ in range(n)]
-    left = [0] * n
-    for i, o in enumerate(ops):
-        for j, w in o["pre"].items():
-            succ[j].append((i, w))
-            left[i] += 1
+    pred = [list(o["pre"].items()) for o in ops]
+    for i in range(n):
+        for j, w in pred[i]: succ[j].append((i, w))
+    cost, lat, hop = [], [], []
+    for C in COSTS:
+        cost.append([o["f"][0] + C["cy"] * (o["f"][1] + C["ga"] * o["f"][2] + C["sc"] * o["f"][3]) + C["pe"] * o["f"][4] for o in ops])
+        lat.append([o["lat"][0] * C["dma"] + o["lat"][1] / C["bw"] + o["lat"][2] * C["rem"] for o in ops])
+        hop.append((C["wake"], C["same"]))
+
+    def length(order, s):
+        c, la, (wk, sm) = cost[s], lat[s], hop[s]
+        fin, sta, free, end = [0.0] * n, [0.0] * n, {}, 0.0
+        for i in order:
+            q = que[i]
+            t = free.get(q, 0.0)
+            for j, w in pred[i]:
+                a = (fin[j] + (sm if que[j] == q else wk)) if w else sta[j]
+                if a > t: t = a
+            sta[i] = t
+            free[q] = t + c[i]
+            fin[i] = t + c[i] + la[i]
+            if fin[i] > end: end = fin[i]
+        return end
+
     pri = [0.0] * n
     for i in range(n - 1, -1, -1):
-        o = ops[i]
+        pri[i] = cost[0][i] + lat[0][i]
         for k, w in succ[i]:
-            d = o["cost"] + (o["lat"] + COST["wake" if ops[k]["q"] != o["q"] else "same"] if w else 0)
+            d = cost[0][i] + (lat[0][i] + hop[0][que[k] == que[i]] if w else 0)
             if d + pri[k] > pri[i]: pri[i] = d + pri[k]
-        if not succ[i]: pri[i] = o["cost"] + o["lat"]
-    amp = 0.0 if seed == 0 else 1500.0 * rand()
-    key = [p + amp * (rand() - 0.5) for p in pri]
-    look = 0.0 if seed == 0 else 300.0 * rand()
-    ready = {}
-    rt = [0.0] * n
-    free = {}
-    for i in range(n):
-        if not left[i]: ready.setdefault(ops[i]["q"], []).append(i)
-    order = []
-    end = 0.0
-    while len(order) < n:
-        bq, bt = None, 1e18
-        for q, L in ready.items():
-            if L:
-                t = max(free.get(q, 0.0), min(rt[i] for i in L))
-                if t < bt: bq, bt = q, t
-        L = ready[bq]
-        best = max((i for i in L if rt[i] <= bt + look), key=lambda i: key[i])
-        L.remove(best)
-        o = ops[best]
-        s = max(bt, rt[best])
-        e = s + o["cost"]
-        free[bq] = e
-        order.append(best)
-        end = max(end, e + o["lat"])
-        for k, w in succ[best]:
-            a = e + o["lat"] + COST["wake" if ops[k]["q"] != bq else "same"] if w else s
-            if a > rt[k]: rt[k] = a
-            left[k] -= 1
-            if not left[k]: ready.setdefault(ops[k]["q"], []).append(k)
-    return end, order
+
+    def greedy(key, look):
+        c, la, (wk, sm) = cost[0], lat[0], hop[0]
+        left = [len(p) for p in pred]
+        ready, rt, free, order = {}, [0.0] * n, {}, []
+        for i in range(n):
+            if not left[i]: ready.setdefault(que[i], []).append(i)
+        while len(order) < n:
+            bq, bt = None, 1e18
+            for q, L in ready.items():
+                if L:
+                    t = max(free.get(q, 0.0), min([rt[i] for i in L]))
+                    if t < bt: bq, bt = q, t
+            L = ready[bq]
+            best = max([i for i in L if rt[i] <= bt + look], key=lambda i: key[i])
+            L.remove(best)
+            s = max(bt, rt[best])
+            e = s + c[best]
+            free[bq] = e
+            order.append(best)
+            e += la[best]
+            for k, w in succ[best]:
+                a = (e + (sm if que[k] == bq else wk)) if w else s
+                if a > rt[k]: rt[k] = a
+                left[k] -= 1
+                if not left[k]: ready.setdefault(que[k], []).append(k)
+        return order
+
+    best = (1e18, None, None, 0.0)
+    for it in range(TRIALS):
+        if it <= TRIALS // 5:
+            amp = 0.0 if it == 0 else 2000.0 * rand()
+            key = [p + amp * (rand() - 0.5) for p in pri]
+            look = 0.0 if it == 0 else 400.0 * rand()
+        else:
+            key, look = list(best[2]), best[3]
+            share = 0.01 if rand() < 0.5 else 0.06
+            for i in range(n):
+                if rand() < share: key[i] += 4000.0 * (rand() - 0.5)
+            if rand() < 0.2: look = 400.0 * rand()
+        order = greedy(key, look)
+        if it == 0: base = [length(order, s) for s in range(len(COSTS))]
+        e = sum([length(order, s) / base[s] for s in range(len(COSTS))])
+        if e < best[0]: best = (e, order, key, look)
+    return length(best[1], 0), best[1]
 
 
 def make(g, T):
@@ -107,7 +143,7 @@ def make(g, T):
         b, c0, c1, s, p0, p1 = r
         return T[b][p0:p1, c0:c1] if s == 1 else T[b][p0:p1, c0:c1:s]
 
-    def add(q, outs, ins, call, cost, lat=0.0, sem=None, inc=1, extra=()):
+    def add(q, outs, ins, call, f, lat=(0, 0, 0), sem=None, inc=1, extra=()):
         i = len(ops)
         acc = []
         for r in ins:
@@ -135,16 +171,16 @@ def make(g, T):
             elif w and not ps and r[3] == 1:
                 h[:] = [a for a in h if a[0] == i or not (a[1][1] >= r[1] and a[1][2] <= r[2] and a[1][4] >= r[4] and a[1][5] <= r[5])]
             h.append((i, r, w))
-        ops.append(dict(q=q, call=call, cost=float(cost), lat=float(lat), pre=pre, sem=sem or own.get(q), inc=inc))
+        ops.append(dict(q=q, call=call, f=tuple(f) + (0,) * (5 - len(f)), lat=lat, pre=pre, sem=sem or own.get(q), inc=inc))
         return i
 
     def sc(x): return ap(x) if isinstance(x, tuple) else x
 
     def vcost(out, in_, f):
         n = wid(out)
-        if len(out) == 3: return 50 + n * COST["sc"] * COST["cy"]
-        if len(in_) == 3: return 50 + n * COST["ga"] * COST["cy"]
-        return max(64, n * f) * COST["cy"]
+        if len(out) == 3: return (50, 0, 0, n)
+        if len(in_) == 3: return (50, 0, n)
+        return (0, max(64, n * f))
 
     def half(*rs): return 0.5 if all(kind(r) in TWO for r in rs) else 1.0
 
@@ -164,20 +200,22 @@ def make(g, T):
     def fill(out, v): add("V", [out], [], lambda n: n.memset(ap(out), v), vcost(out, out, half(out)))
 
     def act(out, in_, f, bias=0.0, scale=1.0, acc=None):
-        c = 65 + wid(out) * COST["ga"] * COST["cy"] if len(in_) == 3 else max(64, wid(out)) * COST["cy"]
+        c = (65, 0, wid(out)) if len(in_) == 3 else (0 if acc is None else 20, max(64, wid(out)))
         if acc is None: add("S", [out], [in_, bias, scale], lambda n: n.activation(ap(out), ap(in_), f, bias=sc(bias), scale=sc(scale)), c)
-        else: add("S", [out, acc], [in_, bias, scale], lambda n: n.activation(ap(out), ap(in_), f, bias=sc(bias), scale=sc(scale), accum_out=ap(acc)), c + 20)
+        else: add("S", [out, acc], [in_, bias, scale], lambda n: n.activation(ap(out), ap(in_), f, bias=sc(bias), scale=sc(scale), accum_out=ap(acc)), c)
 
     def mm(*group):
         def call(n):
             for (o, l, r, a, b) in group:
                 x = n.matmul(ap(o), ap(l), ap(r), a, b)
             return x
-        c = sum(max(min(64, wid(l)), wid(r)) * (4 if kind(l) == "float32" else 1) for (o, l, r, a, b) in group) * COST["pe"]
-        add("P", [x[0] for x in group], [x[1] for x in group] + [x[2] for x in group], call, c)
+        c = sum(max(min(64, wid(l)), wid(r)) * (4 if kind(l) == "float32" else 1) for (o, l, r, a, b) in group)
+        add("P", [x[0] for x in group], [x[1] for x in group] + [x[2] for x in group], call, (0, 0, 0, 0, c))
 
-    def iota(out, pat, base, cm): add("G", [out], [], lambda n: n.iota(ap(out), pat, base, cm, allow_small_or_imprecise_dtypes=True), 130 + 2 * wid(out))
-    def asel(out, in_, pat, o, fillv, base, cm): add("G", [out], [in_], lambda n: n.affine_select(ap(out), ap(in_), pat, o, fillv, base, cm), 170 + 2 * wid(out))
+    def iota(out, pat, base, cm): add("G", [out], [], lambda n: n.iota(ap(out), pat, base, cm, allow_small_or_imprecise_dtypes=True), (130, 2 * wid(out)))
+    def asel(out, in_, pat, o, fillv, base, cm): add("G", [out], [in_], lambda n: n.affine_select(ap(out), ap(in_), pat, o, fillv, base, cm), (170, 2 * wid(out)))
+
+    def cast(out, in_): asel(out, in_, [[0, wid(out)]], ALU.is_gt, 0.0, 1, 0)
 
     nd = [0]
 
@@ -188,18 +226,17 @@ def make(g, T):
         i = T[in_][:] if isinstance(in_, str) else ap(in_)
         s = in_ if isinstance(out, str) else out
         by = wid(s) * 128 * (2 if kind(s) in TWO else 4)
-        add(q, [] if isinstance(out, str) else [out], [] if isinstance(in_, str) else [in_], lambda n: n.dma_start(o, i), 60, COST["dma"] + by / 200.0, sem, 16)
+        add(q, [] if isinstance(out, str) else [out], [] if isinstance(in_, str) else [in_], lambda n: n.dma_start(o, i), (60,), (1, by, 0), sem, 16)
 
     def send(out, in_, rsem, dst, src, topo):
         rid, pid, _ = topo.addr(dst)
         en = topo.engines(src, dst)[:8]
-        i = add("G", [], [in_], lambda n: n.remote_dma(ap(out), ap(in_), T.sem[rsem], T.sem["ls"], pid, rid, sum(1 << x for x in en)), 1000, COST["rem"], "ls", len(en))
-        add("net", [out], [], None, 0, 0, rsem, len(en), (i,))
+        i = add("G", [], [in_], lambda n: n.remote_dma(ap(out), ap(in_), T.sem[rsem], T.sem["ls"], pid, rid, sum(1 << x for x in en)), (1000,), (0, 0, 1), "ls", len(en))
+        add("net", [out], [], None, (0,), (0, 0, 0), rsem, len(en), (i,))
 
     def run():
         if not ORDER:
-            best = min((schedule(ops, s) for s in range(TRIALS)), key=lambda x: x[0])
-            ORDER["best"] = best
+            ORDER["best"] = schedule(ops)
         cnt, known, tok = {}, {q: {} for q in eng}, {}
         for i in ORDER["best"][1]:
             o = ops[i]
@@ -223,7 +260,7 @@ def make(g, T):
         for s in sorted(cnt):
             if known["G"].get(s, 0) < cnt[s]: g.wait_ge(T.sem[s], cnt[s])
 
-    return dict(cp=cp, tt=tt, ts=ts, scan=scan, fill=fill, act=act, mm=mm, iota=iota, asel=asel, dma=dma, send=send, run=run)
+    return dict(cp=cp, tt=tt, ts=ts, scan=scan, fill=fill, act=act, mm=mm, iota=iota, asel=asel, cast=cast, dma=dma, send=send, run=run)
 
 
 def rank_program(g, core, T, topo):
@@ -232,12 +269,14 @@ def rank_program(g, core, T, topo):
         return
     n = len(T.cores)
     m = make(g, T)
-    cp, tt, ts, scan, fill, act, mm, iota, asel, dma = (m[k] for k in ("cp", "tt", "ts", "scan", "fill", "act", "mm", "iota", "asel", "dma"))
+    cp, tt, ts, scan, fill, act, mm, iota, asel, cast, dma = (m[k] for k in ("cp", "tt", "ts", "scan", "fill", "act", "mm", "iota", "asel", "cast", "dma"))
     F = lambda b: R(b, 0, SCRATCH[b][1][1])
     C = lambda b, i=0: R(b, i, i + 1)
     S8 = lambda i: R("WLF", 8 * i, 8 * i + 8)
     K8 = lambda i: R("KJ", 8 * i, 8 * i + 8)
     D8 = lambda b: R(b, 0, 8)
+    G8 = lambda i: R("G8", 8 * i, 8 * i + 8)
+    C8 = G8(2)
     PU, PP, PQ, PZ = R("p0", 0, 128), R("p0", 128, 256), R("p0", 256, 384), R("p0", 384, 512)
     KEY, E8, REC8, AA = R("p1", 0, 128), R("p1", 128, 136), R("p1", 136, 144), R("p1", 144, 145)
     CNT, CNB, JJB = R("p3", 128, 256), R("p3", 256, 384), R("p3", 384, 512)
@@ -247,7 +286,7 @@ def rank_program(g, core, T, topo):
     WI, WL, WX, WG = F("IX"), F("LK"), F("XC"), F("GI")
 
     dma("Y", F("Z0"), "zc"); dma("Y", F("WTI"), "wt"); dma("Y", F("HKI"), "hk")
-    dma("S", R("GI", 0, 1024), "gi"); dma("Y", F("IXI"), "ix"); dma("Y", F("LKI"), "lk"); dma("S", F("XC"), "xc"); dma("Y", F("THI"), "th")
+    dma("S", R("GI", 0, 1024), "gi"); dma("Y", F("IXI"), "ix"); dma("Y", F("THI"), "th"); dma("S", F("XC"), "xc"); dma("Y", F("LKI"), "lk")
 
     fill(F("ONES"), 1.0)
     iota(F("PIO"), [[0, 16]], 0, 1)
@@ -258,7 +297,7 @@ def rank_program(g, core, T, topo):
     iota(F("CIO"), [[1, 8]], 0, 0)
     asel(F("SHF"), F("ONES"), [[-1, 128]], ALU.is_equal, 0.0, -1, 1)
     asel(F("UT"), F("BOF"), [[1, 128]], ALU.is_ge, 0.0, 0, -1)
-    fill(F("ZS"), 0.0)
+    fill(R("ZS", 512, 1536), 0.0)
     for h in (0, 1):
         fill(R("RX", 1024 * h, 1024 * h + 1024), 1.0)
     fill(R("RX", 0, 2048, 16), 0.0)
@@ -267,7 +306,7 @@ def rank_program(g, core, T, topo):
     for q in (0, 3, 1, 2):
         asel(R("RM", 512 * q, 512 * q + 512), F("ONESB"), [[-1, 32], [0, 16]], ALU.is_equal, 0.0, -32 * q, 1)
     for c in range(8):
-        asel(R("R1", SEG[c], SEG[c + 1]), R("ONESB", 0, 16 * c + 16), [[-1, 16 * c + 16]], ALU.is_equal, 0.0, 0, 1)
+        act(R("R1", SEG[c], SEG[c + 1]), R("IDF", 0, 16 * c + 16), ACT.Copy)
     ts(F("PR"), F("PIO"), 15, ALU.bitwise_and)
     act(F("BOB"), F("BOF"), ACT.Copy)
     cp(C("RF"), C("PR"))
@@ -286,14 +325,11 @@ def rank_program(g, core, T, topo):
     ts(F("QWI"), F("QWI"), 2047, ALU.bitwise_and)
     cp(F("PW"), F("PWI"))
     cp(F("QW"), F("QWI"))
-    ts(R("MK", 0, 16), R("RQ", 0, 16), C("RF"), ALU.is_equal)
     ts(F("M16"), F("RQ"), C("RF"), ALU.is_equal)
     ts(F("RMIN"), F("RQ"), 0.0, ALU.is_equal, 3.0e7, ALU.mult)
     ts(F("RMAX"), F("RMIN"), -2.0, ALU.mult, 3.0e7, ALU.add)
-    act(F("G8A"), R("BOF", 0, 128, 16), ACT.Copy, scale=16384.0)
-    act(F("G8B"), R("BOF", 0, 128, 16), ACT.Copy, scale=32768.0)
-    act(F("C8"), R("BOF", 0, 128, 16), ACT.Copy)
-    act(F("C8H"), R("BOF", 0, 128, 16), ACT.Copy, scale=-0.5)
+    for i, v in enumerate((16384.0, 32768.0, 1.0, -0.5, None, -16384.0, 65536.0, -32768.0)):
+        if v is not None: act(G8(i), R("BOF", 0, 128, 16), ACT.Copy, scale=v)
     cp(F("OFFG"), F("CIO"))
     act(F("MROW"), F("RQ"), ACT.Copy, scale=1024.0)
     ts(C("JJC"), C("RF"), -2048.0, ALU.mult, 30720.0, ALU.add)
@@ -302,9 +338,10 @@ def rank_program(g, core, T, topo):
     fill(R("GI", 1024, 1152), 0.0)
     fill(R("XG", 2048, 2064), 0.0)
     act(F("M16B"), F("M16"), ACT.Copy)
-    for k in range(16):
-        act(R("SEL", 128 * k, 128 * k + 128), F("IDF"), ACT.Copy, scale=C("MK", k))
-    act(R("EB", 15, 143, 16), R("BOF", 0, 128, 16), ACT.Copy)
+    for k in range(0, 16, 4):
+        asel(R("SEL", 128 * k, 128 * k + 512), F("ONESB"), [[-1, 4], [-1024, 8], [-63, 16]], ALU.is_equal, 0.0, -k, 64)
+    for at, v in ((0, 1.0), (144, 2.0), (288, -1.0)):
+        act(R("EB", at + 15, at + 143, 16), R("BOF", 0, 128, 16), ACT.Copy, scale=v)
     ts(D8("NC8"), R("BOF", 0, 128, 16), -1.0, ALU.mult)
     for c in range(8):
         act(R("R2", SEG[c], SEG[c + 1]), R("ONESB", 0, 16 * c + 16), ACT.Copy, scale=C("NC8", c))
@@ -331,16 +368,20 @@ def rank_program(g, core, T, topo):
     act(F("IDK"), F("IDF"), ACT.Copy, scale=512.0)
     act(F("NID4K"), F("IDF"), ACT.Copy, scale=-4096.0)
     act(F("SHB"), F("SHF"), ACT.Copy)
-    fill(F("EIGHT"), -7.0)
+    fill(G8(4), -7.0)
     fill(F("M24"), -16777216.0)
     fill(F("HALF"), 0.5)
     fill(C("M95"), -9.5)
-    cp(R("IX", 0, 1024), F("IXI"))
+    for h in (0, 512):
+        cast(R("IX", h, h + 512), R("IXI", h, h + 512))
 
     def ustage(t):
         z = F("Z%d" % t)
-        mm((PU, F("WB"), z, True, True), (PP, F("PW"), z, True, True), (PQ, F("QW"), z, True, True))
+        if t: mm((PU, F("WB"), z, True, True), (PP, F("PW"), z, True, True), (PQ, F("QW"), z, True, True))
+        else: mm((PU, F("WB"), z, True, True))
         cp(F("UI"), PU)
+        if not t: mm((PP, F("PW"), z, True, True))
+        if not t: mm((PQ, F("QW"), z, True, True))
         ts(F("UI"), F("UI"), 4095, ALU.bitwise_and)
         tt(F("UU"), F("UI"), F("UI"), ALU.mult)
         ts(F("S5"), F("UU"), 5, ALU.arith_shift_right, 1023, ALU.bitwise_and)
@@ -349,7 +390,7 @@ def rank_program(g, core, T, topo):
         tt(F("VQ"), PQ, F("VQ"), ALU.add)
         ts(F("VQ"), F("VQ"), 2047, ALU.bitwise_and)
         cp(F("VH"), F("VQ"))
-        cp(R("ZS", 0, 2048, 16), z)
+        cp(R("ZS", 512, 1536, 16), R("Z%d" % t, 32, 96))
         scan(R("ZREP", 512, 1536), R("RX", 512, 1536), R("ZS", 512, 1536), ALU.mult, ALU.add)
         mm((R("p0", 384, 512), z, F("NIDB"), True, True))
         act(F("ZT%d" % (t & 1)), R("p0", 384, 512), ACT.Copy)
@@ -361,41 +402,57 @@ def rank_program(g, core, T, topo):
             b = F("EI")
         ts(F("EM"), b, 1023, ALU.bitwise_and)
         cp(F("EU"), F("EM"))
-        cp(F("MKEY"), F("EM"))
+        cast(F("MKEY"), F("EM"))
         mm((KEY, F("MKEY"), F("IDF"), True, False))
 
     def zsub(p, t, a, b): return (p, F("ZT%d" % (t & 1)), R("RM", a, b), True, False)
 
     def dist(win, off, sub, sh, who, t=None):
-        bank = ["p2", "p5"]
+        bank = ["p2", "p5" if sub == "ZREP" else "p6"]
+        DG, AG = ("DG", "AG") if sub == "ZREP" else ("DY", "AY")
         for q in range(4):
             a, b = 512 * q, 512 * q + 512
             if who[q] == "S":
                 p = bank.pop(0)
-                x = 512 * (p == "p5")
+                x = 512 * (p != "p2")
                 act(R("GR", x, x + 512), ind(win, R(off, 32 * q, 32 * q + 32)), ACT.Copy)
                 P = R(p, 0, 512)
                 if sub == "ZREP": mm(zsub(P, t, a, b))
                 else: mm((P, F("NIDB"), R(sub, a + sh, b + sh), True, False))
                 mm((P, F("IDB"), R("GR", x, x + 512), False, True))
-                act(R("AG", a, b), R(p, 0, 512), ACT.Abs)
+                act(R(AG, a, b), R(p, 0, 512), ACT.Abs)
             else:
-                tt(R("DG", a, b), ind(win, R(off, 32 * q, 32 * q + 32)), R(sub, a + sh, b + sh), ALU.subtract)
-                act(R("AG", a, b), R("DG", a, b), ACT.Abs)
+                tt(R(DG, a, b), ind(win, R(off, 32 * q, 32 * q + 32)), R(sub, a + sh, b + sh), ALU.subtract)
+                if who[q] == "V": act(R(AG, a, b), R(DG, a, b), ACT.Abs)
+                else: ts(R(AG, a, b), R(DG, a, b), 0.0, ALU.max)
+
+    def runs(who):
+        out = []
+        for q in range(4):
+            w = who[q] == "W"
+            if q % 2 and out[-1][2] == w: out[-1] = (out[-1][0], q + 1, w)
+            else: out.append((q, q + 1, w))
+        return out
+
+    def lanesum(out, who, pieces, ks, one, two, neg):
+        for (a, b, w) in pieces:
+            x = "G" if out[0] == "p1" else "Y"
+            for (buf, wt) in ((("D" + x, neg), ("A" + x, two)) if w else (("A" + x, one),)):
+                mm(*[(R(out[0], out[1] + k, out[1] + 128, 16, 32 * a, 32 * b), R(buf, 512 * a + k, 512 * b, 16), wt, False, False) for k in ks])
 
     def gstage(t):
-        dist(WG, "EU", "ZREP", 0, "SVVS", t)
-        for q in (0, 1, 2, 3):
-            mm(*[(R("p1", k, 128, 16, 32 * q, 32 * q + 32), R("AG", 512 * q + k, 512 * q + 512, 16), F("G8A"), False, False) for k in range(16)])
+        dist(WG, "EU", "ZREP", 0, GW, t)
+        for q in GO:
+            lanesum(("p1", 0), GW, [(q, q + 1, GW[q] == "W")], range(16), G8(0), G8(1), G8(5))
         mm((KEY, F("IDB"), F("MROW"), False, True))
 
     def argstage(t):
         scan(F("KMIN"), F("RMIN"), KEY, ALU.max, ALU.min)
         ts(F("KA"), R("KMIN", 15, 128, 16), 1023, ALU.bitwise_and)
         tt(F("ERM"), ind(F("KA"), F("OFFG")), F("M16"), ALU.mult)
-        mm((E8, F("ERM"), F("C8"), True, True))
+        mm((E8, F("ERM"), C8, True, True))
         cp(F("E8U"), E8)
-        cp(F("JU"), ind(WI, F("E8U")))
+        cp(F("JU"), ind(F("IXI") if t == 0 else WI, F("E8U")))
         act(F("JJ%d" % (t & 1)), ind(WI, F("E8U")), ACT.Identity, bias=C("JJC"))
         cp(F("JH"), F("JU"))
 
@@ -446,17 +503,20 @@ def rank_program(g, core, T, topo):
             act(R("AF", a, b), P, ACT.Abs)
 
     def ystage(t):
-        dist(WX, "NU", "XG", 1, "VSVV")
-        for h in (0, 1):
-            mm(*[(R("p4", 128 + 64 * h, 192 + 64 * h), R("EB", 15 - k, 143 - k), R("AG", 1024 * h + k, 1024 * h + 1024, 16), k == 0, k == 14) for k in range(15)])
+        dist(WX, "NU", "XG", 1, YW)
+        for (a, b, w) in runs(YW):
+            o = R("p4", 128 + 32 * a, 128 + 32 * b)
+            src = (("DY", 288), ("AY", 144)) if w else (("AY", 0),)
+            for i, (buf, at) in enumerate(src):
+                mm(*[(o, R("EB", at + 15 - k, at + 143 - k), R(buf, 512 * a + k, 512 * b, 16), i == 0 and k == 0, i == len(src) - 1 and k == 14) for k in range(15)])
 
     def rec(t):
         ts(F("CMP"), ST, C("ACOL"), ALU.is_le)
         if t < RO - 1:
             mm((CNT, F("IDB"), F("MNEG"), True, False), (CNT, F("CMP"), F("BOB"), False, True))
             act(F("RECS"), CNT, ACT.Sign, bias=C("M95"), acc=F("ACC"))
-            mm((REC8, F("IDB"), F("EIGHT"), True, False), (REC8, F("RECS"), F("C8H"), False, True), (AA, F("HALF"), F("ACC"), True, True))
-        mm((CN8, F("CMP"), F("C8"), True, True))
+            mm((REC8, F("IDB"), G8(4), True, False), (REC8, F("RECS"), G8(3), False, True), (AA, F("HALF"), F("ACC"), True, True))
+        mm((CN8, F("CMP"), C8, True, True))
         mm((CNB, F("BOB"), F("CMP"), True, True))
 
     def gists(t):
@@ -478,17 +538,19 @@ def rank_program(g, core, T, topo):
 
     def links(t):
         JJ = F("JJ%d" % (t & 1))
-        mm((PZ, F("IDB"), F("M24"), True, False),
-           *([(R("p0", 384 + k, 512, 16), R("AG", k, 2048, 16), F("G8B"), False, False) for k in range(15)] + [(PZ, JJ, F("IDF"), False, True)]))
+        mm((PZ, F("IDB"), F("M24"), True, False))
+        lanesum(("p0", 384), YW, runs(YW), range(15), G8(1), G8(6), G8(7))
+        mm((PZ, JJ, F("IDF"), False, True))
         scan(F("KMX"), F("RMAX"), PZ, ALU.min, ALU.max)
         ts(K8(0), R("KMX", 15, 128, 16), 32767, ALU.bitwise_and)
         ts(K8(1), R("KMX", 15, 128, 16), 2047, ALU.bitwise_and)
         ts(S8(5), CN8, 10.0, ALU.is_ge, 2048.0, ALU.mult)
         tt(K8(2), K8(1), S8(5), ALU.max)
-        cp(F("REP2"), ind(K8(0), F("OFFG")))
+        cast(S8(7), K8(0))
+        act(F("REP2"), ind(S8(7), F("OFFG")), ACT.Copy)
         mm((JJB, F("REP2"), F("IDF"), True, True))
         tt(F("ERM2"), ind(K8(2), F("OFFG")), F("M16"), ALU.mult)
-        mm((J8, F("ERM2"), F("C8"), True, True))
+        mm((J8, F("ERM2"), C8, True, True))
         cp(F("ERU2"), ind(K8(2), F("OFFG")))
         pairs("ERM2", "ERU2")
         tt(F("NOH"), JJB, JJ, ALU.not_equal)
@@ -509,8 +571,8 @@ def rank_program(g, core, T, topo):
         argstage(t)
         lkx(t)
         if t == 0:
-            for h in (0, 1024):
-                cp(R("LK", h, h + 1024), R("LKI", h, h + 1024))
+            for h in range(0, 2048, 512):
+                cast(R("LK", h, h + 512), R("LKI", h, h + 512))
         idx(t)
         znext(t)
         ystage(t)

from concourse.mybir import AluOpType, ActivationFunctionType

ALU = AluOpType
ACT = ActivationFunctionType
RO = 3
SEG = [8 * c * (c + 1) for c in range(9)]
PSUM = ("p0", "p1", "p2", "p3", "p4", "p5", "p6", "p7")
SCRATCH = {b: ("psum", [128, 512], "float32") for b in PSUM}
for _t, _names in {
    "float32": "IX:1152 LK:2192 ONES:128 IDF:128 BOF:128 SHF:128 HALF:128 RQ:128 M16:128 RMIN:128 RMAX:128 UT:128 MKEY:128 JJ0:128 JJ1:128 ACC:1 WLF:64 SG:128 HV:128 "
               "NT:128 REP2:128 NOH:128 JN:128 TOLD:128",
    "bfloat16": "XC:2048 GI:1152 Z0:128 Z1:128 Z2:128 ZR:128 ZN0:128 ZN1:128 ZN2:128 ZH:128 ZS:2048 ZREP:2048 ZT0:128 ZT1:128 RM:2048 ONESB:512 IDB:128 NIDB:128 HID:128 NHID:128 IDK:128 "
                "NID4K:128 BOB:128 SHB:128 EB:432 G8:64 MROW:128 M24:128 M16B:128 MNEG:128 SEL:2048 RX:2048 RD:576 R1:576 R2:576 R3:576 WB:128 "
                "DG:2048 AG:2048 DY:2048 AY:2048 GR:1024 XG:2064 XM:2048 CMP:128 RECS:128 RBS:128 XA:576 XS:576 AF:2048 NOHB:128",
    "float16": "PD:128 QD:128 PW:128 QW:128 VH:128 ERM:128 ERU:128 ERM2:128 ERU2:128 JH:128 LG:2048",
    "int32": "IXI:1024 LKI:2048 WTI:1 HKI:2 THI:2 PIO:16 PR:16 CIO:8 PWI:128 QWI:128 UI:128 UU:128 S5:128 BS:128 VQ:128 EI:128 EM:128 KMIN:128 KA:8 KMX:128 KJ:24",
    "uint16": "OFFG:8 ENDS:2 EU:128 E8U:8 JU:128 NU:128 GOFF:8 NOFF:8 LOFF:8 JX8:8",
}.items():
    for _n in _names.split():
        SCRATCH[_n.split(":")[0]] = ("sbuf", [128, int(_n.split(":")[1])], _t)
PART = {}
_at = 0
for _n in "RF:1 WC:1 HKF:2 ACOL:1 BCOL:1 THF:2 JJC:1 NM15:1 M95:1 ENDF:4 MK:16 NC8:8 DUMPI:8 DUMPL:8".split():
    PART[_n.split(":")[0]] = _at
    _at += int(_n.split(":")[1])
SCRATCH["CF"] = ("sbuf", [128, _at], "float32")
SEMAPHORES = ["sv", "ss", "sp", "sg", "ls", "za1", "za2", "zr"] + ["d%d" % i for i in range(14)]
TWO = ("bfloat16", "float16", "uint16")
COSTS = [dict(cy=1.0, pe=0.5, ga=1.5, sc=3.0, wake=60.0, same=40.0, dma=2000.0, bw=200.0, rem=2500.0),
         dict(cy=0.9, pe=0.5, ga=1.15, sc=2.0, wake=110.0, same=60.0, dma=2000.0, bw=250.0, rem=3500.0),
         dict(cy=1.15, pe=0.6, ga=1.95, sc=5.0, wake=60.0, same=40.0, dma=2200.0, bw=150.0, rem=2000.0)]
TRIALS = 5000
GW, GO, YW = "SWWS", (1, 0, 2, 3), "SVVV"
ORDER = {}


def R(buf, c0, c1, step=1, p0=0, p1=128):
    if buf in PART:
        return ("CF", PART[buf] + c0, PART[buf] + c1, step, p0, p1)
    return (buf, c0, c1, step, p0, p1)


def ind(win, off): return ("ind", win, off)
def wid(r): return 16 * (r[2][2] - r[2][1]) if len(r) == 3 else (r[2] - r[1] + r[3] - 1) // r[3]
def kind(r): return SCRATCH[(r[1] if len(r) == 3 else r)[0]][2]


def schedule(ops):
    n = len(ops)
    rnd = [12345]

    def rand():
        rnd[0] = (rnd[0] * 1103515245 + 12345) & 0x7fffffff
        return (rnd[0] >> 8) / 0x7fffff

    que = [o["q"] for o in ops]
    succ = [[] for _ in range(n)]
    pred = [list(o["pre"].items()) for o in ops]
    for i in range(n):
        for j, w in pred[i]: succ[j].append((i, w))
    cost, lat, hop = [], [], []
    for C in COSTS:
        cost.append([o["f"][0] + C["cy"] * (o["f"][1] + C["ga"] * o["f"][2] + C["sc"] * o["f"][3]) + C["pe"] * o["f"][4] for o in ops])
        lat.append([o["lat"][0] * C["dma"] + o["lat"][1] / C["bw"] + o["lat"][2] * C["rem"] for o in ops])
        hop.append((C["wake"], C["same"]))

    def length(order, s):
        c, la, (wk, sm) = cost[s], lat[s], hop[s]
        fin, sta, free, end = [0.0] * n, [0.0] * n, {}, 0.0
        for i in order:
            q = que[i]
            t = free.get(q, 0.0)
            for j, w in pred[i]:
                a = (fin[j] + (sm if que[j] == q else wk)) if w else sta[j]
                if a > t: t = a
            sta[i] = t
            free[q] = t + c[i]
            fin[i] = t + c[i] + la[i]
            if fin[i] > end: end = fin[i]
        return end

    pri = [0.0] * n
    for i in range(n - 1, -1, -1):
        pri[i] = cost[0][i] + lat[0][i]
        for k, w in succ[i]:
            d = cost[0][i] + (lat[0][i] + hop[0][que[k] == que[i]] if w else 0)
            if d + pri[k] > pri[i]: pri[i] = d + pri[k]

    def greedy(key, look):
        c, la, (wk, sm) = cost[0], lat[0], hop[0]
        left = [len(p) for p in pred]
        ready, rt, free, order = {}, [0.0] * n, {}, []
        for i in range(n):
            if not left[i]: ready.setdefault(que[i], []).append(i)
        while len(order) < n:
            bq, bt = None, 1e18
            for q, L in ready.items():
                if L:
                    t = max(free.get(q, 0.0), min([rt[i] for i in L]))
                    if t < bt: bq, bt = q, t
            L = ready[bq]
            best = max([i for i in L if rt[i] <= bt + look], key=lambda i: key[i])
            L.remove(best)
            s = max(bt, rt[best])
            e = s + c[best]
            free[bq] = e
            order.append(best)
            e += la[best]
            for k, w in succ[best]:
                a = (e + (sm if que[k] == bq else wk)) if w else s
                if a > rt[k]: rt[k] = a
                left[k] -= 1
                if not left[k]: ready.setdefault(que[k], []).append(k)
        return order

    best = (1e18, None, None, 0.0)
    for it in range(TRIALS):
        if it <= TRIALS // 5:
            amp = 0.0 if it == 0 else 2000.0 * rand()
            key = [p + amp * (rand() - 0.5) for p in pri]
            look = 0.0 if it == 0 else 400.0 * rand()
        else:
            key, look = list(best[2]), best[3]
            share = 0.01 if rand() < 0.5 else 0.06
            for i in range(n):
                if rand() < share: key[i] += 4000.0 * (rand() - 0.5)
            if rand() < 0.2: look = 400.0 * rand()
        order = greedy(key, look)
        if it == 0: base = [length(order, s) for s in range(len(COSTS))]
        e = sum([length(order, s) / base[s] for s in range(len(COSTS))])
        if e < best[0]: best = (e, order, key, look)
    return length(best[1], 0), best[1]


def make(g, T):
    eng = {"V": g.vector, "S": g.scalar, "P": g.tensor, "G": g, "Y": g.sync}
    own = {"V": "sv", "S": "ss", "P": "sp", "G": "sg"}
    ops, hist = [], {}

    def ap(r):
        if len(r) == 3:
            return ap(r[1]).indirect(ap(r[2]))
        b, c0, c1, s, p0, p1 = r
        return T[b][p0:p1, c0:c1] if s == 1 else T[b][p0:p1, c0:c1:s]

    def add(q, outs, ins, call, f, lat=(0, 0, 0), sem=None, inc=1, extra=()):
        i = len(ops)
        acc = []
        for r in ins:
            if isinstance(r, tuple):
                acc += [(r[1], False), (r[2], False)] if len(r) == 3 else [(r, False)]
        for r in outs:
            acc += [(r[1], True), (r[2], False)] if len(r) == 3 else [(r, True)]
        pre = {j: True for j in extra}
        for r, w in acc:
            ps = r[0] in PSUM
            h = hist.setdefault(r[0], [])
            for (j, r2, w2) in h:
                if j == i: continue
                q2 = ops[j]["q"]
                if ps:
                    if q == q2 == "P": wait = False
                    elif q == q2 and not (w or w2): continue
                    else: wait = not (q == q2 and not w2)
                else:
                    if not (w or w2) or r[1] >= r2[2] or r2[1] >= r[2] or r[4] >= r2[5] or r2[4] >= r[5]: continue
                    if r[3] == r2[3] and r[3] > 1 and (r[1] - r2[1]) % r[3]: continue
                    wait = not (q == q2 and not w2)
                pre[j] = pre.get(j, False) or wait
            if ps and q == "P": h[:] = []
            elif w and not ps and r[3] == 1:
                h[:] = [a for a in h if a[0] == i or not (a[1][1] >= r[1] and a[1][2] <= r[2] and a[1][4] >= r[4] and a[1][5] <= r[5])]
            h.append((i, r, w))
        ops.append(dict(q=q, call=call, f=tuple(f) + (0,) * (5 - len(f)), lat=lat, pre=pre, sem=sem or own.get(q), inc=inc))
        return i

    def sc(x): return ap(x) if isinstance(x, tuple) else x

    def vcost(out, in_, f):
        n = wid(out)
        if len(out) == 3: return (50, 0, 0, n)
        if len(in_) == 3: return (50, 0, n)
        return (0, max(64, n * f))

    def half(*rs): return 0.5 if all(kind(r) in TWO for r in rs) else 1.0

    def cp(out, in_): add("V", [out], [in_], lambda n: n.tensor_copy(ap(out), ap(in_)), vcost(out, in_, half(out, in_)))

    def tt(out, a, b, o):
        add("V", [out], [a, b], lambda n: n.tensor_tensor(ap(out), ap(a), ap(b), o), vcost(out, a, 1.0 if a[0] in PSUM or b[0] in PSUM else 2.0))

    def ts(out, a, s1, o1, s2=None, o2=None):
        c = vcost(out, a, half(out, a))
        if o2 is None: add("V", [out], [a, s1], lambda n: n.tensor_scalar(ap(out), ap(a), sc(s1), None, o1), c)
        else: add("V", [out], [a, s1, s2], lambda n: n.tensor_scalar(ap(out), ap(a), sc(s1), sc(s2), o1, o2), c)

    def scan(out, a, b, o1, o2):
        add("V", [out], [a, b], lambda n: n.tensor_tensor_scan(ap(out), ap(a), ap(b), 0.0, o1, o2), vcost(out, a, half(out, a, b)))

    def fill(out, v): add("V", [out], [], lambda n: n.memset(ap(out), v), vcost(out, out, half(out)))

    def act(out, in_, f, bias=0.0, scale=1.0, acc=None):
        c = (65, 0, wid(out)) if len(in_) == 3 else (0 if acc is None else 20, max(64, wid(out)))
        if acc is None: add("S", [out], [in_, bias, scale], lambda n: n.activation(ap(out), ap(in_), f, bias=sc(bias), scale=sc(scale)), c)
        else: add("S", [out, acc], [in_, bias, scale], lambda n: n.activation(ap(out), ap(in_), f, bias=sc(bias), scale=sc(scale), accum_out=ap(acc)), c)

    def mm(*group):
        def call(n):
            for (o, l, r, a, b) in group:
                x = n.matmul(ap(o), ap(l), ap(r), a, b)
            return x
        c = sum(max(min(64, wid(l)), wid(r)) * (4 if kind(l) == "float32" else 1) for (o, l, r, a, b) in group)
        add("P", [x[0] for x in group], [x[1] for x in group] + [x[2] for x in group], call, (0, 0, 0, 0, c))

    def iota(out, pat, base, cm): add("G", [out], [], lambda n: n.iota(ap(out), pat, base, cm, allow_small_or_imprecise_dtypes=True), (130, 2 * wid(out)))
    def asel(out, in_, pat, o, fillv, base, cm): add("G", [out], [in_], lambda n: n.affine_select(ap(out), ap(in_), pat, o, fillv, base, cm), (170, 2 * wid(out)))

    def cast(out, in_): asel(out, in_, [[0, wid(out)]], ALU.is_gt, 0.0, 1, 0)

    nd = [0]

    def dma(q, out, in_):
        sem = "d%d" % nd[0]
        nd[0] += 1
        o = T[out][:] if isinstance(out, str) else ap(out)
        i = T[in_][:] if isinstance(in_, str) else ap(in_)
        s = in_ if isinstance(out, str) else out
        by = wid(s) * 128 * (2 if kind(s) in TWO else 4)
        add(q, [] if isinstance(out, str) else [out], [] if isinstance(in_, str) else [in_], lambda n: n.dma_start(o, i), (60,), (1, by, 0), sem, 16)

    def send(out, in_, rsem, dst, src, topo):
        rid, pid, _ = topo.addr(dst)
        en = topo.engines(src, dst)[:8]
        i = add("G", [], [in_], lambda n: n.remote_dma(ap(out), ap(in_), T.sem[rsem], T.sem["ls"], pid, rid, sum(1 << x for x in en)), (1000,), (0, 0, 1), "ls", len(en))
        add("net", [out], [], None, (0,), (0, 0, 0), rsem, len(en), (i,))

    def run():
        if not ORDER:
            ORDER["best"] = schedule(ops)
        cnt, known, tok = {}, {q: {} for q in eng}, {}
        for i in ORDER["best"][1]:
            o = ops[i]
            q = o["q"]
            cnt[o["sem"]] = cnt.get(o["sem"], 0) + o["inc"]
            if q == "net":
                tok[i] = (o["sem"], cnt[o["sem"]], {})
                continue
            k = known[q]
            waits = sorted((tok[j] for j, w in o["pre"].items() if w), key=lambda t: (t[0], -t[1]))
            waits.sort(key=lambda t: t[0] == o["sem"])
            for (s, v, snap) in waits:
                if k.get(s, 0) < v:
                    eng[q].wait_ge(T.sem[s], v)
                    k[s] = v
                    for a, b in snap.items():
                        if k.get(a, 0) < b: k[a] = b
            c = o["call"](eng[q])
            if o["sem"] != "ls": c.then_inc(T.sem[o["sem"]], o["inc"])
            tok[i] = (o["sem"], cnt[o["sem"]], dict(k))
        for s in sorted(cnt):
            if known["G"].get(s, 0) < cnt[s]: g.wait_ge(T.sem[s], cnt[s])

    return dict(cp=cp, tt=tt, ts=ts, scan=scan, fill=fill, act=act, mm=mm, iota=iota, asel=asel, cast=cast, dma=dma, send=send, run=run)


def rank_program(g, core, T, topo):
    rank = T.rank_of(core)
    if rank is None:
        return
    n = len(T.cores)
    m = make(g, T)
    cp, tt, ts, scan, fill, act, mm, iota, asel, cast, dma = (m[k] for k in ("cp", "tt", "ts", "scan", "fill", "act", "mm", "iota", "asel", "cast", "dma"))
    F = lambda b: R(b, 0, SCRATCH[b][1][1])
    C = lambda b, i=0: R(b, i, i + 1)
    S8 = lambda i: R("WLF", 8 * i, 8 * i + 8)
    K8 = lambda i: R("KJ", 8 * i, 8 * i + 8)
    D8 = lambda b: R(b, 0, 8)
    G8 = lambda i: R("G8", 8 * i, 8 * i + 8)
    C8 = G8(2)
    PU, PP, PQ, PZ = R("p0", 0, 128), R("p0", 128, 256), R("p0", 256, 384), R("p0", 384, 512)
    KEY, E8, REC8, AA = R("p1", 0, 128), R("p1", 128, 136), R("p1", 136, 144), R("p1", 144, 145)
    CNT, CNB, JJB = R("p3", 128, 256), R("p3", 256, 384), R("p3", 384, 512)
    ST, FT = R("p4", 128, 256), R("p4", 256, 384)
    J8, CN8 = R("p7", 96, 104), R("p7", 104, 112)
    HP, DP, JNP = R("p7", 128, 256), R("p7", 256, 384), R("p7", 384, 512)
    WI, WL, WX, WG = F("IX"), F("LK"), F("XC"), F("GI")

    dma("Y", F("Z0"), "zc"); dma("Y", F("WTI"), "wt"); dma("Y", F("HKI"), "hk")
    dma("S", R("GI", 0, 1024), "gi"); dma("Y", F("IXI"), "ix"); dma("Y", F("THI"), "th"); dma("S", F("XC"), "xc"); dma("Y", F("LKI"), "lk")

    fill(F("ONES"), 1.0)
    iota(F("PIO"), [[0, 16]], 0, 1)
    asel(F("IDF"), F("ONES"), [[-1, 128]], ALU.is_equal, 0.0, 0, 1)
    asel(F("BOF"), F("ONES"), [[-16, 8], [0, 16]], ALU.is_ge, 0.0, 0, 1)
    asel(F("BOF"), F("BOF"), [[16, 8], [0, 16]], ALU.is_ge, 0.0, 15, -1)
    iota(F("RQ"), [[0, 8], [1, 16]], 0, 0)
    iota(F("CIO"), [[1, 8]], 0, 0)
    asel(F("SHF"), F("ONES"), [[-1, 128]], ALU.is_equal, 0.0, -1, 1)
    asel(F("UT"), F("BOF"), [[1, 128]], ALU.is_ge, 0.0, 0, -1)
    fill(R("ZS", 512, 1536), 0.0)
    for h in (0, 1):
        fill(R("RX", 1024 * h, 1024 * h + 1024), 1.0)
    fill(R("RX", 0, 2048, 16), 0.0)
    fill(F("ONESB"), 1.0)
    fill(F("EB"), 0.0)
    for q in (0, 3, 1, 2):
        asel(R("RM", 512 * q, 512 * q + 512), F("ONESB"), [[-1, 32], [0, 16]], ALU.is_equal, 0.0, -32 * q, 1)
    for c in range(8):
        act(R("R1", SEG[c], SEG[c + 1]), R("IDF", 0, 16 * c + 16), ACT.Copy)
    ts(F("PR"), F("PIO"), 15, ALU.bitwise_and)
    act(F("BOB"), F("BOF"), ACT.Copy)
    cp(C("RF"), C("PR"))
    act(F("IDB"), F("IDF"), ACT.Copy)
    act(F("NIDB"), F("IDF"), ACT.Copy, scale=-1.0)
    cp(C("WC"), C("WTI"))
    ts(F("WB"), F("BOF"), C("WC"), ALU.mult)
    cp(R("HKF", 0, 2), F("HKI"))
    ts(F("PD"), F("IDF"), C("HKF", 0), ALU.mult)
    ts(F("QD"), F("IDF"), C("HKF", 1), ALU.mult)
    PA, PB = R("p1", 128, 256), R("p1", 256, 384)
    mm((PA, F("BOB"), F("PD"), True, True), (PB, F("BOB"), F("QD"), True, True))
    ts(F("PWI"), PA, C("WC"), ALU.mult)
    ts(F("QWI"), PB, C("WC"), ALU.mult)
    ts(F("PWI"), F("PWI"), 1023, ALU.bitwise_and)
    ts(F("QWI"), F("QWI"), 2047, ALU.bitwise_and)
    cp(F("PW"), F("PWI"))
    cp(F("QW"), F("QWI"))
    ts(F("M16"), F("RQ"), C("RF"), ALU.is_equal)
    ts(F("RMIN"), F("RQ"), 0.0, ALU.is_equal, 3.0e7, ALU.mult)
    ts(F("RMAX"), F("RMIN"), -2.0, ALU.mult, 3.0e7, ALU.add)
    for i, v in enumerate((16384.0, 32768.0, 1.0, -0.5, None, -16384.0, 65536.0, -32768.0)):
        if v is not None: act(G8(i), R("BOF", 0, 128, 16), ACT.Copy, scale=v)
    cp(F("OFFG"), F("CIO"))
    act(F("MROW"), F("RQ"), ACT.Copy, scale=1024.0)
    ts(C("JJC"), C("RF"), -2048.0, ALU.mult, 30720.0, ALU.add)
    fill(R("IX", 1024, 1152), 0.0)
    fill(R("LK", 2048, 2192), 0.0)
    fill(R("GI", 1024, 1152), 0.0)
    fill(R("XG", 2048, 2064), 0.0)
    act(F("M16B"), F("M16"), ACT.Copy)
    for k in range(0, 16, 4):
        asel(R("SEL", 128 * k, 128 * k + 512), F("ONESB"), [[-1, 4], [-1024, 8], [-63, 16]], ALU.is_equal, 0.0, -k, 64)
    for at, v in ((0, 1.0), (144, 2.0), (288, -1.0)):
        act(R("EB", at + 15, at + 143, 16), R("BOF", 0, 128, 16), ACT.Copy, scale=v)
    ts(D8("NC8"), R("BOF", 0, 128, 16), -1.0, ALU.mult)
    for c in range(8):
        act(R("R2", SEG[c], SEG[c + 1]), R("ONESB", 0, 16 * c + 16), ACT.Copy, scale=C("NC8", c))
    fill(F("R3"), 0.0)
    for c in range(8):
        act(R("R3", SEG[c + 1] - 16, SEG[c + 1]), R("UT", 16 * c, 16 * c + 16), ACT.Copy, scale=4096.0)
    fill(F("RD"), 0.0)
    for c in range(8):
        fill(C("RD", SEG[c]), 1.0e6)
    ts(C("ENDF", 0), C("RF"), 7.0, ALU.min)
    ts(C("ENDF", 1), C("ENDF", 0), 8.0, ALU.mult, 24.0, ALU.add)
    tt(C("ENDF", 2), C("ENDF", 0), C("ENDF", 1), ALU.mult)
    ts(C("ENDS"), C("ENDF", 2), 15.0, ALU.add)
    ts(D8("DUMPI"), F("CIO"), 16.0, ALU.mult, C("RF"), ALU.add)
    ts(D8("DUMPL"), D8("DUMPI"), 2049.0, ALU.add)
    ts(D8("DUMPI"), D8("DUMPI"), 1024.0, ALU.add)
    ts(F("MNEG"), F("M16"), 128.0, ALU.mult, -128.0, ALU.add)
    cp(R("THF", 0, 2), F("THI"))
    ts(C("NM15"), C("RF"), 15.0, ALU.is_equal, 2000.0, ALU.mult)
    tt(C("ACOL"), C("THF", 0), C("NM15"), ALU.subtract)
    ts(C("BCOL"), C("THF", 1), -1.0, ALU.mult, 1023.5, ALU.add)
    act(F("HID"), F("IDF"), ACT.Copy, scale=0.5)
    act(F("NHID"), F("IDF"), ACT.Copy, scale=-0.5)
    act(F("IDK"), F("IDF"), ACT.Copy, scale=512.0)
    act(F("NID4K"), F("IDF"), ACT.Copy, scale=-4096.0)
    act(F("SHB"), F("SHF"), ACT.Copy)
    fill(G8(4), -7.0)
    fill(F("M24"), -16777216.0)
    fill(F("HALF"), 0.5)
    fill(C("M95"), -9.5)
    for h in (0, 512):
        cast(R("IX", h, h + 512), R("IXI", h, h + 512))

    def ustage(t):
        z = F("Z%d" % t)
        if t: mm((PU, F("WB"), z, True, True), (PP, F("PW"), z, True, True), (PQ, F("QW"), z, True, True))
        else: mm((PU, F("WB"), z, True, True))
        cp(F("UI"), PU)
        if not t: mm((PP, F("PW"), z, True, True))
        if not t: mm((PQ, F("QW"), z, True, True))
        ts(F("UI"), F("UI"), 4095, ALU.bitwise_and)
        tt(F("UU"), F("UI"), F("UI"), ALU.mult)
        ts(F("S5"), F("UU"), 5, ALU.arith_shift_right, 1023, ALU.bitwise_and)
        tt(F("BS"), PP, F("S5"), ALU.add)
        ts(F("VQ"), F("UU"), 4, ALU.arith_shift_right, 2047, ALU.bitwise_and)
        tt(F("VQ"), PQ, F("VQ"), ALU.add)
        ts(F("VQ"), F("VQ"), 2047, ALU.bitwise_and)
        cp(F("VH"), F("VQ"))
        cp(R("ZS", 512, 1536, 16), R("Z%d" % t, 32, 96))
        scan(R("ZREP", 512, 1536), R("RX", 512, 1536), R("ZS", 512, 1536), ALU.mult, ALU.add)
        mm((R("p0", 384, 512), z, F("NIDB"), True, True))
        act(F("ZT%d" % (t & 1)), R("p0", 384, 512), ACT.Copy)

    def estage(t):
        b = F("BS")
        if t:
            ts(F("EI"), b, AA, ALU.add, 8192.0, ALU.add)
            b = F("EI")
        ts(F("EM"), b, 1023, ALU.bitwise_and)
        cp(F("EU"), F("EM"))
        cast(F("MKEY"), F("EM"))
        mm((KEY, F("MKEY"), F("IDF"), True, False))

    def zsub(p, t, a, b): return (p, F("ZT%d" % (t & 1)), R("RM", a, b), True, False)

    def dist(win, off, sub, sh, who, t=None):
        bank = ["p2", "p5" if sub == "ZREP" else "p6"]
        DG, AG = ("DG", "AG") if sub == "ZREP" else ("DY", "AY")
        for q in range(4):
            a, b = 512 * q, 512 * q + 512
            if who[q] == "S":
                p = bank.pop(0)
                x = 512 * (p != "p2")
                act(R("GR", x, x + 512), ind(win, R(off, 32 * q, 32 * q + 32)), ACT.Copy)
                P = R(p, 0, 512)
                if sub == "ZREP": mm(zsub(P, t, a, b))
                else: mm((P, F("NIDB"), R(sub, a + sh, b + sh), True, False))
                mm((P, F("IDB"), R("GR", x, x + 512), False, True))
                act(R(AG, a, b), R(p, 0, 512), ACT.Abs)
            else:
                tt(R(DG, a, b), ind(win, R(off, 32 * q, 32 * q + 32)), R(sub, a + sh, b + sh), ALU.subtract)
                if who[q] == "V": act(R(AG, a, b), R(DG, a, b), ACT.Abs)
                else: ts(R(AG, a, b), R(DG, a, b), 0.0, ALU.max)

    def runs(who):
        out = []
        for q in range(4):
            w = who[q] == "W"
            if q % 2 and out[-1][2] == w: out[-1] = (out[-1][0], q + 1, w)
            else: out.append((q, q + 1, w))
        return out

    def lanesum(out, who, pieces, ks, one, two, neg):
        for (a, b, w) in pieces:
            x = "G" if out[0] == "p1" else "Y"
            for (buf, wt) in ((("D" + x, neg), ("A" + x, two)) if w else (("A" + x, one),)):
                mm(*[(R(out[0], out[1] + k, out[1] + 128, 16, 32 * a, 32 * b), R(buf, 512 * a + k, 512 * b, 16), wt, False, False) for k in ks])

    def gstage(t):
        dist(WG, "EU", "ZREP", 0, GW, t)
        for q in GO:
            lanesum(("p1", 0), GW, [(q, q + 1, GW[q] == "W")], range(16), G8(0), G8(1), G8(5))
        mm((KEY, F("IDB"), F("MROW"), False, True))

    def argstage(t):
        scan(F("KMIN"), F("RMIN"), KEY, ALU.max, ALU.min)
        ts(F("KA"), R("KMIN", 15, 128, 16), 1023, ALU.bitwise_and)
        tt(F("ERM"), ind(F("KA"), F("OFFG")), F("M16"), ALU.mult)
        mm((E8, F("ERM"), C8, True, True))
        cp(F("E8U"), E8)
        cp(F("JU"), ind(F("IXI") if t == 0 else WI, F("E8U")))
        act(F("JJ%d" % (t & 1)), ind(WI, F("E8U")), ACT.Identity, bias=C("JJC"))
        cp(F("JH"), F("JU"))

    def lkx(t):
        lk = F("LKI") if t == 0 else WL
        for h in (0, 1):
            L = 1024 * h
            cp(R("LG", L, L + 1024), ind(lk, R("JU", 64 * h, 64 * h + 64)))
            p = R(("p3", "p4")[h], 0, 64)
            mm(*[(p, R("SEL", 128 * k, 128 * k + 128), R("LG", L + k, L + 1024, 16), k == 0, k == 15) for k in range(16)])
            cp(R("NU", 64 * h, 64 * h + 64), p)
        for q in range(4):
            act(R("XG", 512 * q, 512 * q + 512), ind(WX, R("JU", 32 * q, 32 * q + 32)), ACT.Copy)

    def pairs(masked, plain):
        for (a, b, P) in ((0, 512, R("p6", 0, 512)), (512, 576, R("p7", 0, 64))):
            mm((P, F("M16B"), R("R3", a, b), True, False), (P, F(plain), R("R1", a, b), False, False), (P, F(masked), R("R2", a, b), False, True))
            act(R("XA", a, b), P, ACT.Abs)

    def lost(out16):
        scan(F("XS"), F("RD"), F("XA"), ALU.max, ALU.min)
        ts(out16, ind(F("XS"), C("ENDS")), 0.0, ALU.is_le)

    def idx(t):
        cp(F("ERU"), ind(F("KA"), F("OFFG")))
        pairs("ERM", "ERU")
        lost(R("WLF", 16, 32))
        tt(S8(0), S8(2), D8("DUMPI"), ALU.mult)
        tt(S8(0), E8, S8(0), ALU.max)
        cp(F("NOFF"), S8(0))

    def znext(t):
        for h in (0, 1024):
            scan(R("XM", h, h + 1024), R("RX", h, h + 1024), R("XG", h, h + 1024), ALU.mult, ALU.max)
        mm((PZ, F("IDB"), F("Z%d" % t), True, False), (PZ, F("IDB"), R("XM", 15, 2048, 16), False, True))
        act(F("ZH"), PZ, ACT.Copy, bias=129.75, scale=0.5)
        act(F("ZN%d" % t), F("ZH"), ACT.Copy, bias=-130.0)
        if t < RO - 1:
            m["send"](F("Z%d" % (t + 1)), F("ZN%d" % t), "za%d" % (t + 1), T.cores[(rank + 1) % n], core, topo)
        else:
            m["send"](F("ZR"), F("ZN%d" % t), "zr", T.cores[(rank - t) % n], core, topo)

    def far(t):
        P = R("p5", 0, 512)
        for q in range(4):
            a, b = 512 * q, 512 * q + 512
            mm(zsub(P, t, a, b), (P, F("IDB"), R("XG", a, b), False, True))
            act(R("AF", a, b), P, ACT.Abs)

    def ystage(t):
        dist(WX, "NU", "XG", 1, YW)
        for (a, b, w) in runs(YW):
            o = R("p4", 128 + 32 * a, 128 + 32 * b)
            src = (("DY", 288), ("AY", 144)) if w else (("AY", 0),)
            for i, (buf, at) in enumerate(src):
                mm(*[(o, R("EB", at + 15 - k, at + 143 - k), R(buf, 512 * a + k, 512 * b, 16), i == 0 and k == 0, i == len(src) - 1 and k == 14) for k in range(15)])

    def rec(t):
        ts(F("CMP"), ST, C("ACOL"), ALU.is_le)
        if t < RO - 1:
            mm((CNT, F("IDB"), F("MNEG"), True, False), (CNT, F("CMP"), F("BOB"), False, True))
            act(F("RECS"), CNT, ACT.Sign, bias=C("M95"), acc=F("ACC"))
            mm((REC8, F("IDB"), G8(4), True, False), (REC8, F("RECS"), G8(3), False, True), (AA, F("HALF"), F("ACC"), True, True))
        mm((CN8, F("CMP"), C8, True, True))
        mm((CNB, F("BOB"), F("CMP"), True, True))

    def gists(t):
        tt(S8(4), REC8, D8("DUMPI"), ALU.mult)
        tt(F("GOFF"), S8(4), S8(0), ALU.max)
        cp(ind(WG, F("GOFF")), F("Z%d" % t))

    def names(t):
        mm((HP, F("HID"), F("VH"), True, False), (HP, F("HID"), F("JH"), False, True), (DP, F("HID"), F("VH"), True, False), (DP, F("NHID"), F("JH"), False, True))
        act(F("HV"), HP, ACT.Copy)
        act(F("RBS"), CNB, ACT.Sign, bias=C("M95"))
        mm((FT, F("IDK"), F("RBS"), True, False))
        for h in (0, 1):
            mm(*[(R("p4", 256 + 64 * h, 320 + 64 * h), R("EB", 15 - k, 143 - k), R("AF", 1024 * h + k, 1024 * h + 1024, 16), False, False) for k in range(16)])
        mm((FT, F("IDK"), F("RBS"), False, True))
        act(F("SG"), FT, ACT.Sign, bias=C("BCOL"))
        tt(F("NT"), DP, F("SG"), ALU.mult)
        tt(ind(WI, F("NOFF")), F("HV"), F("NT"), ALU.add)

    def links(t):
        JJ = F("JJ%d" % (t & 1))
        mm((PZ, F("IDB"), F("M24"), True, False))
        lanesum(("p0", 384), YW, runs(YW), range(15), G8(1), G8(6), G8(7))
        mm((PZ, JJ, F("IDF"), False, True))
        scan(F("KMX"), F("RMAX"), PZ, ALU.min, ALU.max)
        ts(K8(0), R("KMX", 15, 128, 16), 32767, ALU.bitwise_and)
        ts(K8(1), R("KMX", 15, 128, 16), 2047, ALU.bitwise_and)
        ts(S8(5), CN8, 10.0, ALU.is_ge, 2048.0, ALU.mult)
        tt(K8(2), K8(1), S8(5), ALU.max)
        cast(S8(7), K8(0))
        act(F("REP2"), ind(S8(7), F("OFFG")), ACT.Copy)
        mm((JJB, F("REP2"), F("IDF"), True, True))
        tt(F("ERM2"), ind(K8(2), F("OFFG")), F("M16"), ALU.mult)
        mm((J8, F("ERM2"), C8, True, True))
        cp(F("ERU2"), ind(K8(2), F("OFFG")))
        pairs("ERM2", "ERU2")
        tt(F("NOH"), JJB, JJ, ALU.not_equal)
        act(F("NOHB"), F("NOH"), ACT.Copy)
        mm((JNP, F("SHB"), F("JH"), True, False), (JNP, F("NID4K"), F("NOHB"), False, True))
        act(F("JN"), JNP, ACT.Copy)
        cp(F("JX8"), J8)
        tt(F("TOLD"), ind(WL, F("JX8")), F("NOH"), ALU.mult)
        lost(R("WLF", 16, 32))
        tt(S8(6), S8(2), D8("DUMPL"), ALU.mult)
        tt(F("LOFF"), J8, S8(6), ALU.max)
        tt(ind(WL, F("LOFF")), F("TOLD"), F("JN"), ALU.max)

    ustage(0)
    estage(0)
    for t in range(RO):
        gstage(t)
        argstage(t)
        lkx(t)
        if t == 0:
            for h in range(0, 2048, 512):
                cast(R("LK", h, h + 512), R("LKI", h, h + 512))
        idx(t)
        znext(t)
        ystage(t)
        rec(t)
        if t < RO - 1: gists(t)
        far(t)
        names(t)
        links(t)
        if t < RO - 1:
            ustage(t + 1)
            estage(t + 1)
    dma("S", "yi", R("IX", 0, 1024))
    dma("Y", "yl", R("LK", 0, 2048))
    dma("Y", "yz", F("ZR"))
    m["run"]()
